import numpy as np
import ml_dtypes


def mxq(x, axis, fmt="e4m3"):
    dtype, down = {"e4m3": (ml_dtypes.float8_e4m3fn, 7), "e5m2": (ml_dtypes.float8_e5m2, 14)}[fmt]
    v = np.moveaxis(np.asarray(x, np.float32).astype(ml_dtypes.bfloat16).astype(np.float64), axis, -1)
    blocks = v.reshape(v.shape[:-1] + (-1, 32))
    amax = np.abs(blocks).max(-1, keepdims=True)
    byte = np.maximum(np.where(amax > 0, np.frexp(amax)[1] - 1 + 127, 0) - down, 1)
    scale = np.exp2(byte - 127.0)
    codes = (blocks / scale).astype(np.float32).astype(dtype).astype(np.float64)
    return np.moveaxis((codes * scale).reshape(v.shape), -1, axis)


WIDE = False


def mx_kscale(k):
    if not WIDE:
        return np.ones(k)
    levels = np.array([10, -10, 5, -5, 0])
    if k % 512:
        return np.exp2(np.random.permutation(np.resize(levels, k // 32))).repeat(32)
    a = np.empty((k // 512, 16))
    for p in range(k // 512):
        a[p, :8] = np.random.permutation(np.resize(levels, 8))
        for g in range(8):
            far = levels[np.abs(levels - a[p, g]) >= 10]
            a[p, g + 8] = far[np.random.randint(len(far))]
    return np.exp2(a.ravel()).repeat(32)


def f64(x):
    return np.asarray(x).astype(np.float64)


def striped(idx):
    return np.tile(idx.reshape(-1, 16).T, (8, 1)).astype(np.uint16)


def unstriped(offs):
    return offs[:16].T.reshape(-1).astype(np.int64)


def pack_weight(w):
    k, n = w.shape
    w = f64(np.asarray(w, np.float32).astype(ml_dtypes.bfloat16)).reshape(k // 32, 32, n)
    amax = np.abs(w).max(1)
    byte = np.clip(np.where(amax > 0, np.frexp(amax)[1] - 1 + 127 - 7, 1), 1, 254)
    scaled = (w * np.exp2(127.0 - byte)[:, None, :]).reshape(k, n).astype(np.float32)
    words = np.ascontiguousarray(scaled.reshape(k // 512, 128, 4, n).transpose(0, 1, 3, 2)).astype(ml_dtypes.float8_e4m3fn).view(np.uint8)
    return words, np.ascontiguousarray(byte.astype(np.uint8).reshape(k // 512, 16, n))


def unpack_weight(words, scales):
    g, p, n, _ = words.shape
    vals = np.ascontiguousarray(words).view(ml_dtypes.float8_e4m3fn).astype(np.float64) * np.repeat(np.exp2(scales.astype(np.float64) - 127.0), 8, axis=1)[..., None]
    return vals.transpose(0, 1, 3, 2).reshape(g * 512, n)

def planes(y):
    n, m = y.shape
    v = y.astype(np.float32).astype(ml_dtypes.bfloat16).astype(np.float64).reshape(n // 32, 32, m)
    top = np.abs(v).max(1)
    byte = np.clip(np.where(top > 0, np.frexp(top)[1] - 1 + 127 - 7, 1), 1, 254)
    codes = (v * np.exp2(127.0 - byte)[:, None, :]).reshape(n, m).astype(np.float32).astype(ml_dtypes.float8_e4m3fn).view(np.uint8)
    words = codes.reshape(n // 512, 128, 4, m).transpose(0, 1, 3, 2)
    return np.ascontiguousarray(words), np.ascontiguousarray(byte.astype(np.uint8).reshape(n // 512, 16, m))


K, T, S, V, N = 512, 1024, 512, 256, 512
P = 2 ** 7


def setup_inputs():
    n = np.random.standard_normal
    s = mx_kscale(K)[:, None]
    packed_xT = pack_weight(n((K, T)) * s)
    return {
        "x_words": packed_xT[0],
        "x_scales": packed_xT[1],
        "w1": (n((K, N)) / np.sqrt(K) / s).astype(np.float32),
        "bound": np.tile(np.random.uniform(0.3, 1.2, V), (P, 1)).astype(np.float32),
        "offs": striped(np.random.permutation(T)[:S]),
        "cen": striped(np.random.permutation(S)[:V]),
        "pos1": striped(np.random.permutation(S)[:V]),
        "pos2": striped(np.random.permutation(S)[:V]),
        "pos3": striped(np.random.permutation(S)[:V]),
        "pos4": striped(np.random.permutation(S)[:V]),
    }


def reference(x_words, x_scales, w1, bound, offs, cen, pos1, pos2, pos3, pos4):
    xq = unpack_weight(x_words, x_scales)[:, unstriped(offs)]
    y = mxq(f64(w1), 0, "e4m3").T @ xq
    yc = y[:, unstriped(cen)]
    low = -1.0 * f64(bound)[:1]
    out_0 = yc + (np.maximum(np.minimum(y[:, unstriped(pos1)] - yc, f64(bound)[:1]), low) + np.maximum(np.minimum(y[:, unstriped(pos2)] - yc, f64(bound)[:1]), low) + np.maximum(np.minimum(y[:, unstriped(pos3)] - yc, f64(bound)[:1]), low) + np.maximum(np.minimum(y[:, unstriped(pos4)] - yc, f64(bound)[:1]), low)) / 4
    return (out_0,) + planes(out_0)

@@ -1,0 +1,203 @@
+from contextlib import ExitStack
+
+import concourse.mybir as mybir
+from concourse.masks import make_identity
+
+K, T, S, V, N = 512, 1024, 512, 256, 512
+D = 4
+FLOPS = 2 * K * N * S
+
+F32 = mybir.dt.float32
+BF16 = mybir.dt.bfloat16
+I32 = mybir.dt.int32
+U32 = mybir.dt.uint32
+U16 = mybir.dt.uint16
+U8 = mybir.dt.uint8
+FP8X4 = mybir.dt.float8_e4m3fn_x4
+ALU = mybir.AluOpType
+
+P = 128
+PACK = 4
+HALVES = V // P
+
+
+def tile_picked_huber_none_po_kernel(
+    tc, x_words, x_scales, w1, bound, offs, cen, pos1, pos2, pos3, pos4, out_0, out_1, out_2
+):
+    nc = tc.nc
+    with ExitStack() as ctx:
+        keep = ctx.enter_context(tc.tile_pool(name="keep", bufs=1))
+        work = ctx.enter_context(tc.tile_pool(name="work", bufs=2))
+        psum = ctx.enter_context(tc.psum_pool(name="psum", bufs=1))
+
+        offs_sb = keep.tile([P, S // 16], U16, name="offs_sb")
+        nc.sync.dma_start(offs_sb[:], offs)
+
+        x_scale_table = keep.tile([P, T], U8, name="x_scale_table", align_bytes=64)
+        nc.gpsimd.memset(x_scale_table[:].bitcast(I32), 0)
+        for q in range(4):
+            nc.sync.dma_start(
+                x_scale_table[32 * q : 32 * q + 4, :].bitcast(I32),
+                x_scales[0, 4 * q : 4 * q + 4, :].bitcast(I32),
+            )
+
+        w_rows = w1.rearrange("(p j) c -> p j c", j=PACK)
+        w_lo = keep.tile([P, PACK, N // 2], F32, name="w_lo")
+        w_hi = keep.tile([P, PACK, N // 2], F32, name="w_hi")
+        x_word_table = keep.tile([P, T], I32, name="x_word_table", align_bytes=64)
+        nc.sync.dma_start(w_lo[:], w_rows[:, :, : N // 2])
+        nc.sync.dma_start(x_word_table[:], x_words[0].rearrange("p n t -> p (n t)").bitcast(I32))
+        nc.sync.dma_start(w_hi[:], w_rows[:, :, N // 2 :])
+
+        cen_sb = keep.tile([P, V // 16], U16, name="cen_sb")
+        nc.sync.dma_start(cen_sb[:], cen)
+        pos_sb = []
+        for d, pos in enumerate((pos1, pos2, pos3, pos4)):
+            lst = keep.tile([P, V // 16], U16, name="pos_sb%d" % d)
+            nc.sync.dma_start(lst[:], pos)
+            pos_sb.append(lst)
+
+        upper = keep.tile([P, HALVES], F32, name="upper")
+        with nc.allow_non_contiguous_dma(reason="one bound a partition"):
+            nc.sync.dma_start(upper[:], bound[0].rearrange("(h p) -> p h", p=P))
+        lower = keep.tile([P, HALVES], F32, name="lower")
+        nc.gpsimd.tensor_scalar(lower[:], upper[:], -1.0, 0.0, ALU.mult, ALU.add)
+
+        ident = keep.tile([P, P], F32, name="ident")
+        make_identity(nc, ident[:])
+
+        x_scales_picked = keep.tile([P, S], U8, name="x_scales_picked", align_bytes=64)
+        x_words_picked = keep.tile([P, S], U32, name="x_words_picked", align_bytes=64)
+        nc.vector.tensor_copy(x_scales_picked[:], x_scale_table[:].indirect(offs_sb[:]))
+        nc.vector.tensor_copy(x_words_picked[:], x_word_table[:].bitcast(U32).indirect(offs_sb[:]))
+
+        w_grouped = keep.tile([P, PACK, P, PACK], BF16, name="w_grouped", align_bytes=64)
+        w_dealt = w_grouped[:].rearrange("p t m j -> p m t j")
+        nc.scalar.copy(w_dealt[:, : P // 2], w_lo[:].rearrange("p j (m t) -> p m t j", t=PACK))
+        w_hi_dealt = w_hi[:].rearrange("p j (m t) -> p m t j", t=PACK)
+        SPLIT = 24
+        nc.scalar.copy(w_dealt[:, P // 2 : P // 2 + SPLIT], w_hi_dealt[:, :SPLIT])
+        nc.vector.tensor_copy(w_dealt[:, P // 2 + SPLIT :], w_hi_dealt[:, SPLIT:])
+
+        w_codes = keep.tile([P, N], U32, name="w_codes", align_bytes=64)
+        w_scales = keep.tile([P, N], U8, name="w_scales", align_bytes=64)
+        y = []
+        for t in range(PACK):
+            cols = slice(t * P, (t + 1) * P)
+            nc.vector.quantize_mx(
+                out=w_codes[:, cols].bitcast(FP8X4),
+                scales=w_scales[:, cols],
+                in_=w_grouped[:, t].rearrange("p m j -> p (m j)"),
+            )
+            y_t = keep.tile([P, S], F32, name="y%d" % t)
+            if t == 0:
+                pieces = [(slice(0, S // 2), nc.scalar.copy), (slice(S // 2, S), nc.vector.tensor_copy)]
+            else:
+                pieces = [(slice(0, S), nc.scalar.copy)]
+            for entries, copy_out in pieces:
+                y_bank = psum.tile([P, entries.stop - entries.start], F32, name="y_bank", tag="rows", bufs=6)
+                nc.tensor.matmul_mx(
+                    out=y_bank[:],
+                    lhsT=w_codes[:, cols].bitcast(FP8X4),
+                    lhsT_scale=w_scales[:, cols],
+                    rhs=x_words_picked[:, entries].bitcast(FP8X4),
+                    rhs_scale=x_scales_picked[:, entries],
+                    start=True,
+                    stop=True,
+                )
+                copy_out(y_t[:, entries], y_bank[:])
+            y.append(y_t)
+
+        out_rows = out_0.rearrange("(p t) v -> p t v", t=PACK)
+        out_words = out_1[0].rearrange("p v t -> p (v t)").bitcast(I32)
+        result = keep.tile([P, PACK, V], F32, name="result")
+        out_codes = keep.tile([P, V], U32, name="out_codes", align_bytes=64)
+        out_scales = keep.tile([P, V], U8, name="out_scales", align_bytes=64)
+
+        centre = [keep.tile([P, V], F32, name="centre%d" % t) for t in range(PACK)]
+        neighbour = {}
+
+        def fetch_centre(t):
+            nc.vector.tensor_copy(centre[t][:], y[t][:].indirect(cen_sb[:]))
+
+        def fetch_neighbours(t, halves, ds):
+            entries = slice(halves[0] * P // 16, (halves[-1] + 1) * P // 16)
+            for d in ds:
+                fetched = keep.tile([P, len(halves), P], F32, name="neighbour%d_%d_%d" % (t, halves[0], d))
+                nc.vector.tensor_tensor(
+                    fetched[:].rearrange("p i v -> p (i v)"), y[t][:].indirect(pos_sb[d][:, entries]),
+                    centre[t][:, halves[0] * P : (halves[-1] + 1) * P], ALU.subtract,
+                )
+                for i, h in enumerate(halves):
+                    neighbour[t, h, d] = fetched[:, i]
+
+        batches = []
+        for t in range(PACK - 1):
+            batches.append((t, [0, 1], [0, 1]))
+            batches.append((t, [0, 1], [2, 3]))
+        batches.append((PACK - 1, [0], [0, 1, 2, 3]))
+        batches.append((PACK - 1, [1], [0, 1]))
+        batches.append((PACK - 1, [1], [2, 3]))
+
+        fetch_centre(0)
+        for t, halves, ds in batches:
+            fetch_neighbours(t, halves, ds)
+            if ds[0] == 0 and t + 1 < PACK:
+                fetch_centre(t + 1)
+
+        sum_bank = {}
+
+        def pull(t, halves, ds, last):
+            n = len(halves)
+            if ds[0] == 0:
+                sum_bank[t, halves[0]] = psum.tile([P, n, P], F32, name="sum_bank", tag="rows", bufs=6)
+            total = sum_bank[t, halves[0]]
+            pull_bank = psum.tile([P, n, len(ds), P], F32, name="pull_bank", bufs=2)
+            for e, d in enumerate(ds):
+                for i, h in enumerate(halves):
+                    nc.tensor.transpose(pull_bank[:, i, e], neighbour[t, h, d], ident[:])
+            clipped = work.tile([P, n, len(ds), P], F32, name="clipped", bufs=2)
+            if last:
+                source, clip = pull_bank, nc.vector.tensor_scalar
+            else:
+                source, clip = work.tile([P, n, len(ds), P], F32, name="pull", bufs=2), nc.gpsimd.tensor_scalar
+                nc.scalar.copy(source[:], pull_bank[:])
+            for i, h in enumerate(halves):
+                clip(clipped[:, i], source[:, i], upper[:, h : h + 1], lower[:, h : h + 1], ALU.min, ALU.max)
+                for e, d in enumerate(ds):
+                    nc.tensor.matmul(
+                        total[:, i], clipped[:, i, e], ident[:],
+                        start=(d == 0 and i == 0), stop=(d == D - 1 and i == n - 1), is_transpose=True,
+                    )
+            if ds[-1] == D - 1:
+                targets = slice(halves[0] * P, (halves[-1] + 1) * P)
+                nc.vector.scalar_tensor_tensor(
+                    result[:, t, targets], total[:].rearrange("p i v -> p (i v)"), 1.0 / D, centre[t][:, targets],
+                    ALU.mult, ALU.add,
+                )
+                nc.sync.dma_start(out_rows[:, t, targets], result[:, t, targets])
+
+        def quantise_result(h):
+            targets = slice(h * P, (h + 1) * P)
+            out_grouped = work.tile([P, P, PACK], BF16, name="out_grouped", align_bytes=64)
+            nc.vector.tensor_copy(
+                out_grouped[:].rearrange("p (c i) t -> p c t i", i=4),
+                result[:, :, targets].rearrange("p t (c i) -> p c t i", i=4),
+            )
+            nc.vector.quantize_mx(
+                out=out_codes[:, targets].bitcast(FP8X4),
+                scales=out_scales[:, targets],
+                in_=out_grouped[:].rearrange("p v t -> p (v t)"),
+            )
+            nc.sync.dma_start(out_words[:, targets], out_codes[:, targets].bitcast(I32))
+
+        for t, halves, ds in batches:
+            pull(t, halves, ds, (t, halves, ds) == batches[-1])
+            if t == PACK - 1 and ds[-1] == D - 1:
+                quantise_result(halves[0])
+        for q in range(4):
+            queue = nc.scalar if q % 2 == 0 else nc.sync
+            queue.dma_start(
+                out_2[0, 4 * q : 4 * q + 4, :].bitcast(I32),
+                out_scales[32 * q : 32 * q + 4, :].bitcast(I32),
+            )

@@ -15,10 +15,12 @@ U16 = mybir.dt.uint16
 U8 = mybir.dt.uint8
 FP8X4 = mybir.dt.float8_e4m3fn_x4
 ALU = mybir.AluOpType
+COPY = mybir.ActivationFunctionType.Copy
 
 P = 128
 PACK = 4
 HALVES = V // P
+NB = 3
 
 
 def tile_picked_huber_none_po_kernel(
@@ -30,6 +32,8 @@ def tile_picked_huber_none_po_kernel(
         work = ctx.enter_context(tc.tile_pool(name="work", bufs=2))
         psum = ctx.enter_context(tc.psum_pool(name="psum", bufs=1))
 
+        x_word_table = keep.tile([P, T], I32, name="x_word_table", align_bytes=64)
+        nc.sync.dma_start(x_word_table[:], x_words[0].rearrange("p n t -> p (n t)").bitcast(I32))
         offs_sb = keep.tile([P, S // 16], U16, name="offs_sb")
         nc.sync.dma_start(offs_sb[:], offs)
 
@@ -44,9 +48,7 @@ def tile_picked_huber_none_po_kernel(
         w_rows = w1.rearrange("(p j) c -> p j c", j=PACK)
         w_lo = keep.tile([P, PACK, N // 2], F32, name="w_lo")
         w_hi = keep.tile([P, PACK, N // 2], F32, name="w_hi")
-        x_word_table = keep.tile([P, T], I32, name="x_word_table", align_bytes=64)
         nc.sync.dma_start(w_lo[:], w_rows[:, :, : N // 2])
-        nc.sync.dma_start(x_word_table[:], x_words[0].rearrange("p n t -> p (n t)").bitcast(I32))
         nc.sync.dma_start(w_hi[:], w_rows[:, :, N // 2 :])
 
         cen_sb = keep.tile([P, V // 16], U16, name="cen_sb")
@@ -61,23 +63,22 @@ def tile_picked_huber_none_po_kernel(
         with nc.allow_non_contiguous_dma(reason="one bound a partition"):
             nc.sync.dma_start(upper[:], bound[0].rearrange("(h p) -> p h", p=P))
         lower = keep.tile([P, HALVES], F32, name="lower")
-        nc.gpsimd.tensor_scalar(lower[:], upper[:], -1.0, 0.0, ALU.mult, ALU.add)
+        nc.scalar.activation(lower[:], upper[:], COPY, scale=-1.0)
 
         ident = keep.tile([P, P], F32, name="ident")
         make_identity(nc, ident[:])
 
         x_scales_picked = keep.tile([P, S], U8, name="x_scales_picked", align_bytes=64)
         x_words_picked = keep.tile([P, S], U32, name="x_words_picked", align_bytes=64)
-        nc.vector.tensor_copy(x_scales_picked[:], x_scale_table[:].indirect(offs_sb[:]))
         nc.vector.tensor_copy(x_words_picked[:], x_word_table[:].bitcast(U32).indirect(offs_sb[:]))
+        nc.vector.tensor_copy(x_scales_picked[:], x_scale_table[:].indirect(offs_sb[:]))
 
         w_grouped = keep.tile([P, PACK, P, PACK], BF16, name="w_grouped", align_bytes=64)
         w_dealt = w_grouped[:].rearrange("p t m j -> p m t j")
         nc.scalar.copy(w_dealt[:, : P // 2], w_lo[:].rearrange("p j (m t) -> p m t j", t=PACK))
         w_hi_dealt = w_hi[:].rearrange("p j (m t) -> p m t j", t=PACK)
-        SPLIT = 24
-        nc.scalar.copy(w_dealt[:, P // 2 : P // 2 + SPLIT], w_hi_dealt[:, :SPLIT])
-        nc.vector.tensor_copy(w_dealt[:, P // 2 + SPLIT :], w_hi_dealt[:, SPLIT:])
+        nc.vector.tensor_copy(w_dealt[:, P // 2 :, 0], w_hi_dealt[:, :, 0])
+        nc.scalar.copy(w_dealt[:, P // 2 :, 1:], w_hi_dealt[:, :, 1:])
 
         w_codes = keep.tile([P, N], U32, name="w_codes", align_bytes=64)
         w_scales = keep.tile([P, N], U8, name="w_scales", align_bytes=64)
@@ -95,7 +96,7 @@ def tile_picked_huber_none_po_kernel(
             else:
                 pieces = [(slice(0, S), nc.scalar.copy)]
             for entries, copy_out in pieces:
-                y_bank = psum.tile([P, entries.stop - entries.start], F32, name="y_bank", tag="rows", bufs=6)
+                y_bank = psum.tile([P, entries.stop - entries.start], F32, name="y_bank", tag="rows", bufs=4)
                 nc.tensor.matmul_mx(
                     out=y_bank[:],
                     lhsT=w_codes[:, cols].bitcast(FP8X4),
@@ -115,67 +116,54 @@ def tile_picked_huber_none_po_kernel(
         out_scales = keep.tile([P, V], U8, name="out_scales", align_bytes=64)
 
         centre = [keep.tile([P, V], F32, name="centre%d" % t) for t in range(PACK)]
-        neighbour = {}
+        centre_turned = [keep.tile([P, HALVES, P], F32, name="centre_turned%d" % t) for t in range(PACK)]
 
         def fetch_centre(t):
             nc.vector.tensor_copy(centre[t][:], y[t][:].indirect(cen_sb[:]))
+            centre_bank = psum.tile([P, HALVES, P], F32, name="centre_bank", bufs=1)
+            for h in range(HALVES):
+                nc.tensor.transpose(centre_bank[:, h], centre[t][:, h * P : (h + 1) * P], ident[:])
+            nc.scalar.activation(centre_turned[t][:], centre_bank[:], COPY, scale=float(D))
 
-        def fetch_neighbours(t, halves, ds):
-            entries = slice(halves[0] * P // 16, (halves[-1] + 1) * P // 16)
-            for d in ds:
-                fetched = keep.tile([P, len(halves), P], F32, name="neighbour%d_%d_%d" % (t, halves[0], d))
-                nc.vector.tensor_tensor(
-                    fetched[:].rearrange("p i v -> p (i v)"), y[t][:].indirect(pos_sb[d][:, entries]),
-                    centre[t][:, halves[0] * P : (halves[-1] + 1) * P], ALU.subtract,
-                )
-                for i, h in enumerate(halves):
-                    neighbour[t, h, d] = fetched[:, i]
-
-        batches = []
-        for t in range(PACK - 1):
-            batches.append((t, [0, 1], [0, 1]))
-            batches.append((t, [0, 1], [2, 3]))
-        batches.append((PACK - 1, [0], [0, 1, 2, 3]))
-        batches.append((PACK - 1, [1], [0, 1]))
-        batches.append((PACK - 1, [1], [2, 3]))
-
-        fetch_centre(0)
-        for t, halves, ds in batches:
-            fetch_neighbours(t, halves, ds)
-            if ds[0] == 0 and t + 1 < PACK:
-                fetch_centre(t + 1)
-
-        sum_bank = {}
-
-        def pull(t, halves, ds, last):
-            n = len(halves)
-            if ds[0] == 0:
-                sum_bank[t, halves[0]] = psum.tile([P, n, P], F32, name="sum_bank", tag="rows", bufs=6)
-            total = sum_bank[t, halves[0]]
-            pull_bank = psum.tile([P, n, len(ds), P], F32, name="pull_bank", bufs=2)
+        def fetch_pulls(t, halves, ds):
+            targets = slice(halves[0] * P, (halves[-1] + 1) * P)
+            entries = slice(targets.start // 16, targets.stop // 16)
+            pull_bank = psum.tile([P, len(halves), len(ds), P], F32, name="pull_bank", bufs=3)
             for e, d in enumerate(ds):
-                for i, h in enumerate(halves):
-                    nc.tensor.transpose(pull_bank[:, i, e], neighbour[t, h, d], ident[:])
-            clipped = work.tile([P, n, len(ds), P], F32, name="clipped", bufs=2)
-            if last:
-                source, clip = pull_bank, nc.vector.tensor_scalar
-            else:
-                source, clip = work.tile([P, n, len(ds), P], F32, name="pull", bufs=2), nc.gpsimd.tensor_scalar
-                nc.scalar.copy(source[:], pull_bank[:])
-            for i, h in enumerate(halves):
-                clip(clipped[:, i], source[:, i], upper[:, h : h + 1], lower[:, h : h + 1], ALU.min, ALU.max)
-                for e, d in enumerate(ds):
-                    nc.tensor.matmul(
-                        total[:, i], clipped[:, i, e], ident[:],
-                        start=(d == 0 and i == 0), stop=(d == D - 1 and i == n - 1), is_transpose=True,
-                    )
-            if ds[-1] == D - 1:
-                targets = slice(halves[0] * P, (halves[-1] + 1) * P)
-                nc.vector.scalar_tensor_tensor(
-                    result[:, t, targets], total[:].rearrange("p i v -> p (i v)"), 1.0 / D, centre[t][:, targets],
-                    ALU.mult, ALU.add,
+                pull = work.tile([P, len(halves) * P], F32, name="pull", bufs=NB)
+                nc.vector.tensor_tensor(
+                    pull[:], y[t][:].indirect(pos_sb[d][:, entries]), centre[t][:, targets], ALU.subtract
                 )
-                nc.sync.dma_start(out_rows[:, t, targets], result[:, t, targets])
+                for i in range(len(halves)):
+                    nc.tensor.transpose(pull_bank[:, i, e], pull[:, i * P : (i + 1) * P], ident[:])
+            return pull_bank
+
+        def add_up(t, halves, clipped):
+            total = psum.tile([P, len(halves), P], F32, name="total", tag="rows", bufs=4)
+            for i, h in enumerate(halves):
+                terms = [centre_turned[t][:, h]] + clipped[i]
+                for e, term in enumerate(terms):
+                    nc.tensor.matmul(
+                        total[:, i], term, ident[:], start=(e == 0), stop=(e == len(terms) - 1), is_transpose=True
+                    )
+            targets = slice(halves[0] * P, (halves[-1] + 1) * P)
+            nc.scalar.activation(result[:, t, targets], total[:].rearrange("p i v -> p (i v)"), COPY, scale=1.0 / D)
+            nc.sync.dma_start(out_rows[:, t, targets], result[:, t, targets])
+
+        def smooth(t, halves, batches):
+            n = len(halves)
+            turned = work.tile([P, n, D, P], F32, name="turned", bufs=2)
+            for ds in batches:
+                pull_bank = fetch_pulls(t, halves, ds)
+                nc.scalar.copy(turned[:, :, ds[0] : ds[-1] + 1], pull_bank[:])
+                if ds[0] == 0 and t + 1 < PACK:
+                    fetch_centre(t + 1)
+            clipped = work.tile([P, n, D, P], F32, name="clipped", bufs=2)
+            for i, h in enumerate(halves):
+                nc.vector.tensor_scalar(
+                    clipped[:, i], turned[:, i], upper[:, h : h + 1], lower[:, h : h + 1], ALU.min, ALU.max
+                )
+            add_up(t, halves, [[clipped[:, i, d] for d in range(D)] for i in range(n)])
 
         def quantise_result(h):
             targets = slice(h * P, (h + 1) * P)
@@ -191,10 +179,19 @@ def tile_picked_huber_none_po_kernel(
             )
             nc.sync.dma_start(out_words[:, targets], out_codes[:, targets].bitcast(I32))
 
-        for t, halves, ds in batches:
-            pull(t, halves, ds, (t, halves, ds) == batches[-1])
-            if t == PACK - 1 and ds[-1] == D - 1:
-                quantise_result(halves[0])
+        fetch_centre(0)
+        for t in range(PACK - 1):
+            smooth(t, [0, 1], [[0, 1], [2, 3]])
+        smooth(PACK - 1, [0], [[0, 1, 2, 3]])
+        quantise_result(0)
+        clipped = work.tile([P, D, P], F32, name="clipped", bufs=2)
+        for ds in ([0, 1], [2, 3]):
+            pull_bank = fetch_pulls(PACK - 1, [1], ds)
+            nc.vector.tensor_scalar(
+                clipped[:, ds[0] : ds[-1] + 1], pull_bank[:, 0], upper[:, 1:2], lower[:, 1:2], ALU.min, ALU.max
+            )
+        add_up(PACK - 1, [1], [[clipped[:, d] for d in range(D)]])
+        quantise_result(1)
         for q in range(4):
             queue = nc.scalar if q % 2 == 0 else nc.sync
             queue.dma_start(

@@ -20,7 +20,6 @@ COPY = mybir.ActivationFunctionType.Copy
 P = 128
 PACK = 4
 HALVES = V // P
-NB = 3
 
 
 def tile_picked_huber_none_po_kernel(
@@ -115,60 +114,65 @@ def tile_picked_huber_none_po_kernel(
         out_codes = keep.tile([P, V], U32, name="out_codes", align_bytes=64)
         out_scales = keep.tile([P, V], U8, name="out_scales", align_bytes=64)
 
-        centre = [keep.tile([P, V], F32, name="centre%d" % t) for t in range(PACK)]
-        centre_turned = [keep.tile([P, HALVES, P], F32, name="centre_turned%d" % t) for t in range(PACK)]
+        last = PACK - 1
+        centre, total, turned = {}, {}, {}
 
-        def fetch_centre(t):
+        def slot(t, h):
+            return "slot%d_%d" % (t, h)
+
+        def turn(bank_part, rows, start, stop):
+            nc.tensor.matmul(bank_part, rows, ident[:], start=start, stop=stop, is_transpose=True)
+
+        def fetch_centre(t, halves, tag):
+            centre[t] = keep.tile([P, V], F32, name="centre%d" % t, tag=tag)
             nc.vector.tensor_copy(centre[t][:], y[t][:].indirect(cen_sb[:]))
-            centre_bank = psum.tile([P, HALVES, P], F32, name="centre_bank", bufs=1)
-            for h in range(HALVES):
-                nc.tensor.transpose(centre_bank[:, h], centre[t][:, h * P : (h + 1) * P], ident[:])
-            nc.scalar.activation(centre_turned[t][:], centre_bank[:], COPY, scale=float(D))
+            centre_bank = psum.tile([P, len(halves), P], F32, name="centre_bank", bufs=1)
+            for h in halves:
+                turn(centre_bank[:, h], centre[t][:, h * P : (h + 1) * P], True, True)
+            centre_turned = work.tile([P, len(halves), P], F32, name="centre_turned")
+            nc.scalar.activation(centre_turned[:], centre_bank[:], COPY, scale=float(D))
+            total[t] = psum.tile([P, len(halves), P], F32, name="total", tag="rows", bufs=4)
+            for h in halves:
+                turn(total[t][:, h], centre_turned[:, h], h == 0, False)
 
-        def fetch_pulls(t, halves, ds):
+        def new_bank(halves, count):
+            return psum.tile([P, len(halves), count, P], F32, name="pull_bank", bufs=3)
+
+        def fetch_pull(t, halves, d, bank, e, tag):
             targets = slice(halves[0] * P, (halves[-1] + 1) * P)
             entries = slice(targets.start // 16, targets.stop // 16)
-            pull_bank = psum.tile([P, len(halves), len(ds), P], F32, name="pull_bank", bufs=3)
-            for e, d in enumerate(ds):
-                pull = work.tile([P, len(halves) * P], F32, name="pull", bufs=NB)
-                nc.vector.tensor_tensor(
-                    pull[:], y[t][:].indirect(pos_sb[d][:, entries]), centre[t][:, targets], ALU.subtract
-                )
-                for i in range(len(halves)):
-                    nc.tensor.transpose(pull_bank[:, i, e], pull[:, i * P : (i + 1) * P], ident[:])
-            return pull_bank
+            pull = keep.tile([P, len(halves) * P], F32, name="pull", tag=tag)
+            nc.vector.tensor_tensor(
+                pull[:], y[t][:].indirect(pos_sb[d][:, entries]), centre[t][:, targets], ALU.subtract
+            )
+            for i in range(len(halves)):
+                turn(bank[:, i, e], pull[:, i * P : (i + 1) * P], True, True)
 
-        def add_up(t, halves, clipped):
-            total = psum.tile([P, len(halves), P], F32, name="total", tag="rows", bufs=4)
+        def empty(t, halves, bank, first):
             for i, h in enumerate(halves):
-                terms = [centre_turned[t][:, h]] + clipped[i]
-                for e, term in enumerate(terms):
-                    nc.tensor.matmul(
-                        total[:, i], term, ident[:], start=(e == 0), stop=(e == len(terms) - 1), is_transpose=True
-                    )
-            targets = slice(halves[0] * P, (halves[-1] + 1) * P)
-            nc.scalar.activation(result[:, t, targets], total[:].rearrange("p i v -> p (i v)"), COPY, scale=1.0 / D)
+                if first == 0:
+                    turned[t, h] = keep.tile([P, D, P], F32, name="turned", tag=slot(t, h))
+                nc.scalar.copy(turned[t, h][:, first : first + bank.shape[2]], bank[:, i])
+
+        def clip(out, pulls, h):
+            nc.vector.tensor_scalar(out, pulls, upper[:, h : h + 1], lower[:, h : h + 1], ALU.min, ALU.max)
+
+        def clip_and_add(t, h, stop):
+            clipped = work.tile([P, D, P], F32, name="clipped", bufs=3)
+            clip(clipped[:], turned[t, h][:], h)
+            for d in range(D):
+                turn(total[t][:, h], clipped[:, d], False, stop and d == D - 1)
+
+        def hand_out(t, targets):
+            nc.scalar.activation(
+                result[:, t, targets], total[t][:].rearrange("p h v -> p (h v)"), COPY, scale=1.0 / D
+            )
             nc.sync.dma_start(out_rows[:, t, targets], result[:, t, targets])
 
-        def smooth(t, halves, batches):
-            n = len(halves)
-            turned = work.tile([P, n, D, P], F32, name="turned", bufs=2)
-            for ds in batches:
-                pull_bank = fetch_pulls(t, halves, ds)
-                nc.scalar.copy(turned[:, :, ds[0] : ds[-1] + 1], pull_bank[:])
-                if ds[0] == 0 and t + 1 < PACK:
-                    fetch_centre(t + 1)
-            clipped = work.tile([P, n, D, P], F32, name="clipped", bufs=2)
-            for i, h in enumerate(halves):
-                nc.vector.tensor_scalar(
-                    clipped[:, i], turned[:, i], upper[:, h : h + 1], lower[:, h : h + 1], ALU.min, ALU.max
-                )
-            add_up(t, halves, [[clipped[:, i, d] for d in range(D)] for i in range(n)])
-
-        def quantise_result(h):
+        def quantise_result(h, copy):
             targets = slice(h * P, (h + 1) * P)
             out_grouped = work.tile([P, P, PACK], BF16, name="out_grouped", align_bytes=64)
-            nc.vector.tensor_copy(
+            copy(
                 out_grouped[:].rearrange("p (c i) t -> p c t i", i=4),
                 result[:, :, targets].rearrange("p t (c i) -> p c t i", i=4),
             )
@@ -179,19 +183,56 @@ def tile_picked_huber_none_po_kernel(
             )
             nc.sync.dma_start(out_words[:, targets], out_codes[:, targets].bitcast(I32))
 
-        fetch_centre(0)
-        for t in range(PACK - 1):
-            smooth(t, [0, 1], [[0, 1], [2, 3]])
-        smooth(PACK - 1, [0], [[0, 1, 2, 3]])
-        quantise_result(0)
-        clipped = work.tile([P, D, P], F32, name="clipped", bufs=2)
-        for ds in ([0, 1], [2, 3]):
-            pull_bank = fetch_pulls(PACK - 1, [1], ds)
-            nc.vector.tensor_scalar(
-                clipped[:, ds[0] : ds[-1] + 1], pull_bank[:, 0], upper[:, 1:2], lower[:, 1:2], ALU.min, ALU.max
-            )
-        add_up(PACK - 1, [1], [[clipped[:, d] for d in range(D)]])
-        quantise_result(1)
+        both = [0, 1]
+        fetch_centre(0, both, "centre0")
+        for t in range(last):
+            bank = new_bank(both, 2)
+            for d in (0, 1):
+                fetch_pull(t, both, d, bank, d, "pull%d_%d" % (t, d))
+            empty(t, both, bank, 0)
+            bank = new_bank(both, 2)
+            fetch_pull(t, both, 2, bank, 0, "pull%d_2" % t)
+            if t > 0:
+                clip_and_add(t - 1, 0, False)
+            fetch_centre(t + 1, both if t + 1 < last else [0], slot(t - 1, 0))
+            if t > 0:
+                clip_and_add(t - 1, 1, True)
+            fetch_pull(t, both, 3, bank, 1, slot(t - 1, 1))
+            if t > 0:
+                hand_out(t - 1, slice(0, V))
+            empty(t, both, bank, 2)
+
+        bank = new_bank([0], D)
+        for d in range(D):
+            fetch_pull(last, [0], d, bank, d, "pull%d_%d" % (last, d))
+        empty(last, [0], bank, 0)
+        front_bank = new_bank([1], 2)
+        fetch_pull(last, [1], 0, front_bank, 0, "pull_front")
+        clip_and_add(last - 1, 0, False)
+        fetch_pull(last, [1], 1, front_bank, 1, slot(last - 1, 0))
+        clip_and_add(last - 1, 1, True)
+        back_bank = new_bank([1], 2)
+        fetch_pull(last, [1], 2, back_bank, 0, slot(last - 1, 1))
+        hand_out(last - 1, slice(0, V))
+        clipped = work.tile([P, D, P], F32, name="clipped", bufs=3)
+        clip(clipped[:], turned[last, 0][:], 0)
+        fetch_pull(last, [1], 3, back_bank, 1, slot(last, 0))
+        for d in range(D):
+            turn(total[last][:, 0], clipped[:, d], False, d == D - 1)
+        hand_out(last, slice(0, P))
+
+        clipped = work.tile([P, D, P], F32, name="clipped", bufs=3)
+        clip(clipped[:, :2], front_bank[:, 0], 1)
+        clip(clipped[:, 2:], back_bank[:, 0], 1)
+        end_total = psum.tile([P, P], F32, name="end_total", tag="rows", bufs=4)
+        for d in range(D):
+            turn(end_total[:], clipped[:, d], d == 0, d == D - 1)
+        nc.vector.scalar_tensor_tensor(
+            result[:, last, P:], end_total[:], 1.0 / D, centre[last][:, P:], ALU.mult, ALU.add
+        )
+        nc.sync.dma_start(out_rows[:, last, P:], result[:, last, P:])
+        quantise_result(0, nc.scalar.copy)
+        quantise_result(1, nc.vector.tensor_copy)
         for q in range(4):
             queue = nc.scalar if q % 2 == 0 else nc.sync
             queue.dma_start(

@@ -20,6 +20,9 @@ COPY = mybir.ActivationFunctionType.Copy
 P = 128
 PACK = 4
 HALVES = V // P
+QUADRANTS = 4
+PER_COLUMN = 16
+ROW_BANKS, PULL_BANKS, CENTRE_BANKS = 4, 3, 1
 
 
 def tile_picked_huber_none_po_kernel(
@@ -33,12 +36,12 @@ def tile_picked_huber_none_po_kernel(
 
         x_word_table = keep.tile([P, T], I32, name="x_word_table", align_bytes=64)
         nc.sync.dma_start(x_word_table[:], x_words[0].rearrange("p n t -> p (n t)").bitcast(I32))
-        offs_sb = keep.tile([P, S // 16], U16, name="offs_sb")
+        offs_sb = keep.tile([P, S // PER_COLUMN], U16, name="offs_sb")
         nc.sync.dma_start(offs_sb[:], offs)
 
         x_scale_table = keep.tile([P, T], U8, name="x_scale_table", align_bytes=64)
         nc.gpsimd.memset(x_scale_table[:].bitcast(I32), 0)
-        for q in range(4):
+        for q in range(QUADRANTS):
             nc.sync.dma_start(
                 x_scale_table[32 * q : 32 * q + 4, :].bitcast(I32),
                 x_scales[0, 4 * q : 4 * q + 4, :].bitcast(I32),
@@ -50,13 +53,13 @@ def tile_picked_huber_none_po_kernel(
         nc.sync.dma_start(w_lo[:], w_rows[:, :, : N // 2])
         nc.sync.dma_start(w_hi[:], w_rows[:, :, N // 2 :])
 
-        cen_sb = keep.tile([P, V // 16], U16, name="cen_sb")
+        cen_sb = keep.tile([P, V // PER_COLUMN], U16, name="cen_sb")
         nc.sync.dma_start(cen_sb[:], cen)
         pos_sb = []
         for d, pos in enumerate((pos1, pos2, pos3, pos4)):
-            lst = keep.tile([P, V // 16], U16, name="pos_sb%d" % d)
-            nc.sync.dma_start(lst[:], pos)
-            pos_sb.append(lst)
+            pos_list = keep.tile([P, V // PER_COLUMN], U16, name="pos_sb%d" % d)
+            nc.sync.dma_start(pos_list[:], pos)
+            pos_sb.append(pos_list)
 
         upper = keep.tile([P, HALVES], F32, name="upper")
         with nc.allow_non_contiguous_dma(reason="one bound a partition"):
@@ -91,11 +94,11 @@ def tile_picked_huber_none_po_kernel(
             )
             y_t = keep.tile([P, S], F32, name="y%d" % t)
             if t == 0:
-                pieces = [(slice(0, S // 2), nc.scalar.copy), (slice(S // 2, S), nc.vector.tensor_copy)]
+                pieces = [(slice(0, S // 2), nc.vector.tensor_copy), (slice(S // 2, S), nc.scalar.copy)]
             else:
                 pieces = [(slice(0, S), nc.scalar.copy)]
             for entries, copy_out in pieces:
-                y_bank = psum.tile([P, entries.stop - entries.start], F32, name="y_bank", tag="rows", bufs=4)
+                y_bank = psum.tile([P, entries.stop - entries.start], F32, name="y_bank", tag="rows", bufs=ROW_BANKS)
                 nc.tensor.matmul_mx(
                     out=y_bank[:],
                     lhsT=w_codes[:, cols].bitcast(FP8X4),
@@ -115,7 +118,9 @@ def tile_picked_huber_none_po_kernel(
         out_scales = keep.tile([P, V], U8, name="out_scales", align_bytes=64)
 
         last = PACK - 1
+        both = list(range(HALVES))
         centre, total, turned = {}, {}, {}
+        out_grouped = [keep.tile([P, P, PACK], BF16, name="out_grouped%d" % h, align_bytes=64) for h in both]
 
         def slot(t, h):
             return "slot%d_%d" % (t, h)
@@ -123,30 +128,32 @@ def tile_picked_huber_none_po_kernel(
         def turn(bank_part, rows, start, stop):
             nc.tensor.matmul(bank_part, rows, ident[:], start=start, stop=stop, is_transpose=True)
 
-        def fetch_centre(t, halves, tag):
+        def fetch_centre(t, tag):
             centre[t] = keep.tile([P, V], F32, name="centre%d" % t, tag=tag)
             nc.vector.tensor_copy(centre[t][:], y[t][:].indirect(cen_sb[:]))
-            centre_bank = psum.tile([P, len(halves), P], F32, name="centre_bank", bufs=1)
+
+        def open_total(t, halves, rows, scale):
+            centre_bank = psum.tile([P, len(halves), P], F32, name="centre_bank", bufs=CENTRE_BANKS)
             for h in halves:
-                turn(centre_bank[:, h], centre[t][:, h * P : (h + 1) * P], True, True)
+                turn(centre_bank[:, h], rows[:, h * P : (h + 1) * P], True, True)
             centre_turned = work.tile([P, len(halves), P], F32, name="centre_turned")
-            nc.scalar.activation(centre_turned[:], centre_bank[:], COPY, scale=float(D))
-            total[t] = psum.tile([P, len(halves), P], F32, name="total", tag="rows", bufs=4)
+            nc.scalar.activation(centre_turned[:], centre_bank[:], COPY, scale=scale)
+            total[t] = psum.tile([P, len(halves), P], F32, name="total", tag="rows", bufs=ROW_BANKS)
             for h in halves:
                 turn(total[t][:, h], centre_turned[:, h], h == 0, False)
 
         def new_bank(halves, count):
-            return psum.tile([P, len(halves), count, P], F32, name="pull_bank", bufs=3)
+            return psum.tile([P, len(halves), count, P], F32, name="pull_bank", bufs=PULL_BANKS)
 
-        def fetch_pull(t, halves, d, bank, e, tag):
+        def fetch_pull(t, halves, d, bank, place, tag):
             targets = slice(halves[0] * P, (halves[-1] + 1) * P)
-            entries = slice(targets.start // 16, targets.stop // 16)
+            columns = slice(targets.start // PER_COLUMN, targets.stop // PER_COLUMN)
             pull = keep.tile([P, len(halves) * P], F32, name="pull", tag=tag)
             nc.vector.tensor_tensor(
-                pull[:], y[t][:].indirect(pos_sb[d][:, entries]), centre[t][:, targets], ALU.subtract
+                pull[:], y[t][:].indirect(pos_sb[d][:, columns]), centre[t][:, targets], ALU.subtract
             )
             for i in range(len(halves)):
-                turn(bank[:, i, e], pull[:, i * P : (i + 1) * P], True, True)
+                turn(bank[:, i, place], pull[:, i * P : (i + 1) * P], True, True)
 
         def empty(t, halves, bank, first):
             for i, h in enumerate(halves):
@@ -157,8 +164,11 @@ def tile_picked_huber_none_po_kernel(
         def clip(out, pulls, h):
             nc.vector.tensor_scalar(out, pulls, upper[:, h : h + 1], lower[:, h : h + 1], ALU.min, ALU.max)
 
+        def new_clipped():
+            return work.tile([P, D, P], F32, name="clipped", bufs=3)
+
         def clip_and_add(t, h, stop):
-            clipped = work.tile([P, D, P], F32, name="clipped", bufs=3)
+            clipped = new_clipped()
             clip(clipped[:], turned[t, h][:], h)
             for d in range(D):
                 turn(total[t][:, h], clipped[:, d], False, stop and d == D - 1)
@@ -169,38 +179,54 @@ def tile_picked_huber_none_po_kernel(
             )
             nc.sync.dma_start(out_rows[:, t, targets], result[:, t, targets])
 
-        def quantise_result(h, copy):
-            targets = slice(h * P, (h + 1) * P)
-            out_grouped = work.tile([P, P, PACK], BF16, name="out_grouped", align_bytes=64)
-            copy(
-                out_grouped[:].rearrange("p (c i) t -> p c t i", i=4),
-                result[:, :, targets].rearrange("p t (c i) -> p c t i", i=4),
+        def regroup(h, blocks):
+            nc.scalar.copy(
+                out_grouped[h][:, :, blocks].rearrange("p (c i) t -> p c t i", i=4),
+                result[:, blocks, h * P : (h + 1) * P].rearrange("p t (c i) -> p c t i", i=4),
             )
+
+        def quantise_result(h):
+            targets = slice(h * P, (h + 1) * P)
             nc.vector.quantize_mx(
                 out=out_codes[:, targets].bitcast(FP8X4),
                 scales=out_scales[:, targets],
-                in_=out_grouped[:].rearrange("p v t -> p (v t)"),
+                in_=out_grouped[h][:].rearrange("p v t -> p (v t)"),
             )
             nc.sync.dma_start(out_words[:, targets], out_codes[:, targets].bitcast(I32))
 
-        both = [0, 1]
-        fetch_centre(0, both, "centre0")
-        for t in range(last):
+        fetch_centre(0, "centre0")
+        minus_centre = keep.tile([P, V], F32, name="minus_centre")
+        nc.scalar.activation(minus_centre[:], centre[0][:], COPY, scale=-1.0)
+        for first in (0, 2):
+            bank = new_bank(both, 2)
+            for h in both:
+                for place in range(2):
+                    turn(bank[:, h, place], minus_centre[:, h * P : (h + 1) * P], h == 0 and place == 0, False)
+            for place in range(2):
+                neighbour = keep.tile([P, V], F32, name="neighbour%d" % (first + place))
+                nc.vector.tensor_copy(neighbour[:], y[0][:].indirect(pos_sb[first + place][:]))
+                for h in both:
+                    turn(bank[:, h, place], neighbour[:, h * P : (h + 1) * P], False, h == 1 and place == 1)
+            if first == 0:
+                fetch_centre(1, "centre1")
+            empty(0, both, bank, first)
+        open_total(0, both, minus_centre, -float(D))
+        open_total(1, both, centre[1], float(D))
+
+        for t in range(1, last):
             bank = new_bank(both, 2)
             for d in (0, 1):
                 fetch_pull(t, both, d, bank, d, "pull%d_%d" % (t, d))
             empty(t, both, bank, 0)
             bank = new_bank(both, 2)
             fetch_pull(t, both, 2, bank, 0, "pull%d_2" % t)
-            if t > 0:
-                clip_and_add(t - 1, 0, False)
-            fetch_centre(t + 1, both if t + 1 < last else [0], slot(t - 1, 0))
-            if t > 0:
-                clip_and_add(t - 1, 1, True)
+            clip_and_add(t - 1, 0, False)
+            fetch_centre(t + 1, slot(t - 1, 0))
+            clip_and_add(t - 1, 1, True)
             fetch_pull(t, both, 3, bank, 1, slot(t - 1, 1))
-            if t > 0:
-                hand_out(t - 1, slice(0, V))
+            hand_out(t - 1, slice(0, V))
             empty(t, both, bank, 2)
+            open_total(t + 1, both if t + 1 < last else [0], centre[t + 1], float(D))
 
         bank = new_bank([0], D)
         for d in range(D):
@@ -214,26 +240,30 @@ def tile_picked_huber_none_po_kernel(
         back_bank = new_bank([1], 2)
         fetch_pull(last, [1], 2, back_bank, 0, slot(last - 1, 1))
         hand_out(last - 1, slice(0, V))
-        clipped = work.tile([P, D, P], F32, name="clipped", bufs=3)
+        clipped = new_clipped()
         clip(clipped[:], turned[last, 0][:], 0)
         fetch_pull(last, [1], 3, back_bank, 1, slot(last, 0))
         for d in range(D):
             turn(total[last][:, 0], clipped[:, d], False, d == D - 1)
         hand_out(last, slice(0, P))
 
-        clipped = work.tile([P, D, P], F32, name="clipped", bufs=3)
-        clip(clipped[:, :2], front_bank[:, 0], 1)
-        clip(clipped[:, 2:], back_bank[:, 0], 1)
-        end_total = psum.tile([P, P], F32, name="end_total", tag="rows", bufs=4)
+        end_clipped = keep.tile([P, D, P], F32, name="end_clipped", tag="y%d" % last)
+        clip(end_clipped[:, :2], front_bank[:, 0], 1)
+        clip(end_clipped[:, 2:], back_bank[:, 0], 1)
+        end_total = psum.tile([P, P], F32, name="end_total", tag="rows", bufs=ROW_BANKS)
         for d in range(D):
-            turn(end_total[:], clipped[:, d], d == 0, d == D - 1)
-        nc.vector.scalar_tensor_tensor(
-            result[:, last, P:], end_total[:], 1.0 / D, centre[last][:, P:], ALU.mult, ALU.add
-        )
+            turn(end_total[:], end_clipped[:, d], d == 0, d == D - 1)
+
+        regroup(1, slice(0, 2))
+        regroup(0, slice(0, PACK))
+        nc.vector.tensor_copy(out_grouped[1][:, :, last - 1], result[:, last - 1, P:])
+        for out in (out_grouped[1][:, :, last], result[:, last, P:]):
+            nc.vector.scalar_tensor_tensor(out, end_total[:], 1.0 / D, centre[last][:, P:], ALU.mult, ALU.add)
         nc.sync.dma_start(out_rows[:, last, P:], result[:, last, P:])
-        quantise_result(0, nc.scalar.copy)
-        quantise_result(1, nc.vector.tensor_copy)
-        for q in range(4):
+        quantise_result(1)
+        quantise_result(0)
+
+        for q in range(QUADRANTS):
             queue = nc.scalar if q % 2 == 0 else nc.sync
             queue.dma_start(
                 out_2[0, 4 * q : 4 * q + 4, :].bitcast(I32),

@@ -16,13 +16,14 @@ U8 = mybir.dt.uint8
 FP8X4 = mybir.dt.float8_e4m3fn_x4
 ALU = mybir.AluOpType
 COPY = mybir.ActivationFunctionType.Copy
+RELU = mybir.ActivationFunctionType.Relu
 
 P = 128
 PACK = 4
 HALVES = V // P
 QUADRANTS = 4
 PER_COLUMN = 16
-ROW_BANKS, PULL_BANKS, CENTRE_BANKS = 4, 3, 1
+ROW_BANKS = 5
 
 
 def tile_picked_huber_none_po_kernel(
@@ -55,6 +56,8 @@ def tile_picked_huber_none_po_kernel(
 
         cen_sb = keep.tile([P, V // PER_COLUMN], U16, name="cen_sb")
         nc.sync.dma_start(cen_sb[:], cen)
+        bound_rows = keep.tile([P, V], F32, name="bound_rows")
+        nc.sync.dma_start(bound_rows[:], bound)
         pos_sb = []
         for d, pos in enumerate((pos1, pos2, pos3, pos4)):
             pos_list = keep.tile([P, V // PER_COLUMN], U16, name="pos_sb%d" % d)
@@ -64,8 +67,8 @@ def tile_picked_huber_none_po_kernel(
         upper = keep.tile([P, HALVES], F32, name="upper")
         with nc.allow_non_contiguous_dma(reason="one bound a partition"):
             nc.sync.dma_start(upper[:], bound[0].rearrange("(h p) -> p h", p=P))
-        lower = keep.tile([P, HALVES], F32, name="lower")
-        nc.scalar.activation(lower[:], upper[:], COPY, scale=-1.0)
+        span = keep.tile([P, HALVES], F32, name="span")
+        nc.scalar.activation(span[:], upper[:], COPY, scale=2.0)
 
         ident = keep.tile([P, P], F32, name="ident")
         make_identity(nc, ident[:])
@@ -119,64 +122,51 @@ def tile_picked_huber_none_po_kernel(
 
         last = PACK - 1
         both = list(range(HALVES))
-        centre, total, turned = {}, {}, {}
+        floor, total, slab = {}, {}, {}
         out_grouped = [keep.tile([P, P, PACK], BF16, name="out_grouped%d" % h, align_bytes=64) for h in both]
-
-        def slot(t, h):
-            return "slot%d_%d" % (t, h)
 
         def turn(bank_part, rows, start, stop):
             nc.tensor.matmul(bank_part, rows, ident[:], start=start, stop=stop, is_transpose=True)
 
-        def fetch_centre(t, tag):
-            centre[t] = keep.tile([P, V], F32, name="centre%d" % t, tag=tag)
-            nc.vector.tensor_copy(centre[t][:], y[t][:].indirect(cen_sb[:]))
+        def fetch_floor(t, out):
+            floor[t] = out
+            nc.vector.tensor_tensor(out, y[t][:].indirect(cen_sb[:]), bound_rows[:], ALU.subtract)
 
-        def open_total(t, halves, rows, scale):
-            centre_bank = psum.tile([P, len(halves), P], F32, name="centre_bank", bufs=CENTRE_BANKS)
-            for h in halves:
-                turn(centre_bank[:, h], rows[:, h * P : (h + 1) * P], True, True)
-            centre_turned = work.tile([P, len(halves), P], F32, name="centre_turned")
-            nc.scalar.activation(centre_turned[:], centre_bank[:], COPY, scale=scale)
-            total[t] = psum.tile([P, len(halves), P], F32, name="total", tag="rows", bufs=ROW_BANKS)
-            for h in halves:
-                turn(total[t][:, h], centre_turned[:, h], h == 0, False)
+        def new_bank(tag, count):
+            return psum.tile([P, count, P], F32, name="pull_bank", tag="pulls%d" % tag, bufs=1)
 
-        def new_bank(halves, count):
-            return psum.tile([P, len(halves), count, P], F32, name="pull_bank", bufs=PULL_BANKS)
-
-        def fetch_pull(t, halves, d, bank, place, tag):
+        def fetch_pull(t, halves, d, banks, place):
             targets = slice(halves[0] * P, (halves[-1] + 1) * P)
             columns = slice(targets.start // PER_COLUMN, targets.stop // PER_COLUMN)
-            pull = keep.tile([P, len(halves) * P], F32, name="pull", tag=tag)
-            nc.vector.tensor_tensor(
-                pull[:], y[t][:].indirect(pos_sb[d][:, columns]), centre[t][:, targets], ALU.subtract
-            )
-            for i in range(len(halves)):
-                turn(bank[:, i, place], pull[:, i * P : (i + 1) * P], True, True)
-
-        def empty(t, halves, bank, first):
+            pull = slab[t][:, d, targets]
+            nc.vector.tensor_tensor(pull, y[t][:].indirect(pos_sb[d][:, columns]), floor[t][:, targets], ALU.subtract)
             for i, h in enumerate(halves):
-                if first == 0:
-                    turned[t, h] = keep.tile([P, D, P], F32, name="turned", tag=slot(t, h))
-                nc.scalar.copy(turned[t, h][:, first : first + bank.shape[2]], bank[:, i])
+                turn(banks[i][:, place], slab[t][:, d, h * P : (h + 1) * P], True, True)
 
-        def clip(out, pulls, h):
-            nc.vector.tensor_scalar(out, pulls, upper[:, h : h + 1], lower[:, h : h + 1], ALU.min, ALU.max)
+        def add_up(acc, clipped, count, start, stop):
+            for j in range(count):
+                turn(acc, clipped[:, j], start and j == 0, stop and j == count - 1)
 
-        def new_clipped():
-            return work.tile([P, D, P], F32, name="clipped", bufs=3)
+        def clip_on_scalar(halves, banks, accs, start, stop):
+            count = banks[0].shape[1]
+            rooms = []
+            for i, h in enumerate(halves):
+                room = work.tile([P, count, P], F32, name="room", bufs=4)
+                nc.scalar.activation(room[:], banks[i][:], RELU, bias=span[:, h : h + 1], scale=-1.0)
+                rooms.append(room)
+            for i, h in enumerate(halves):
+                clipped = work.tile([P, count, P], F32, name="clipped", bufs=6)
+                nc.scalar.activation(clipped[:], rooms[i][:], RELU, bias=span[:, h : h + 1], scale=-1.0)
+                add_up(accs[i], clipped, count, start and i == 0, stop and i == len(halves) - 1)
 
-        def clip_and_add(t, h, stop):
-            clipped = new_clipped()
-            clip(clipped[:], turned[t, h][:], h)
-            for d in range(D):
-                turn(total[t][:, h], clipped[:, d], False, stop and d == D - 1)
+        def new_total(halves):
+            return psum.tile([P, len(halves), P], F32, name="total", tag="rows", bufs=ROW_BANKS)
 
-        def hand_out(t, targets):
-            nc.scalar.activation(
-                result[:, t, targets], total[t][:].rearrange("p h v -> p (h v)"), COPY, scale=1.0 / D
-            )
+        def finish(out, acc, t, targets):
+            nc.vector.scalar_tensor_tensor(out, acc, 1.0 / D, floor[t][:, targets], ALU.mult, ALU.add)
+
+        def hand_out(t, acc, targets):
+            finish(result[:, t, targets], acc, t, targets)
             nc.sync.dma_start(out_rows[:, t, targets], result[:, t, targets])
 
         def regroup(h, blocks):
@@ -194,74 +184,60 @@ def tile_picked_huber_none_po_kernel(
             )
             nc.sync.dma_start(out_words[:, targets], out_codes[:, targets].bitcast(I32))
 
-        fetch_centre(0, "centre0")
-        minus_centre = keep.tile([P, V], F32, name="minus_centre")
-        nc.scalar.activation(minus_centre[:], centre[0][:], COPY, scale=-1.0)
-        for first in (0, 2):
-            bank = new_bank(both, 2)
-            for h in both:
-                for place in range(2):
-                    turn(bank[:, h, place], minus_centre[:, h * P : (h + 1) * P], h == 0 and place == 0, False)
-            for place in range(2):
-                neighbour = keep.tile([P, V], F32, name="neighbour%d" % (first + place))
-                nc.vector.tensor_copy(neighbour[:], y[0][:].indirect(pos_sb[first + place][:]))
-                for h in both:
-                    turn(bank[:, h, place], neighbour[:, h * P : (h + 1) * P], False, h == 1 and place == 1)
-            if first == 0:
-                fetch_centre(1, "centre1")
-            empty(0, both, bank, first)
-        open_total(0, both, minus_centre, -float(D))
-        open_total(1, both, centre[1], float(D))
+        def flat(acc):
+            return acc[:].rearrange("p h v -> p (h v)")
 
-        for t in range(1, last):
-            bank = new_bank(both, 2)
+        tags = ["slab_a", "slab_b", "slab_c", "slab_a"]
+        first_floor = keep.tile([P, V], F32, name="first_floor", tag="slab_c")
+        fetch_floor(0, first_floor[:])
+        for t in range(last):
+            slab[t] = keep.tile([P, D + 1, V], F32, name="slab", tag=tags[t])
+            total[t] = new_total(both)
+            accs = [total[t][:, h] for h in both]
+            bank = [new_bank(h, 2) for h in both]
             for d in (0, 1):
-                fetch_pull(t, both, d, bank, d, "pull%d_%d" % (t, d))
-            empty(t, both, bank, 0)
-            bank = new_bank(both, 2)
-            fetch_pull(t, both, 2, bank, 0, "pull%d_2" % t)
-            clip_and_add(t - 1, 0, False)
-            fetch_centre(t + 1, slot(t - 1, 0))
-            clip_and_add(t - 1, 1, True)
-            fetch_pull(t, both, 3, bank, 1, slot(t - 1, 1))
-            hand_out(t - 1, slice(0, V))
-            empty(t, both, bank, 2)
-            open_total(t + 1, both if t + 1 < last else [0], centre[t + 1], float(D))
+                fetch_pull(t, both, d, bank, d)
+            clip_on_scalar(both, bank, accs, True, False)
+            bank = [new_bank(h, 2) for h in both]
+            fetch_pull(t, both, 2, bank, 0)
+            if t == 0:
+                fetch_floor(1, slab[0][:, D])
+            fetch_pull(t, both, 3, bank, 1)
+            if t > 0:
+                fetch_floor(t + 1, slab[t][:, D])
+                hand_out(t - 1, flat(total[t - 1]), slice(0, V))
+            clip_on_scalar(both, bank, accs, False, True)
 
-        bank = new_bank([0], D)
-        for d in range(D):
-            fetch_pull(last, [0], d, bank, d, "pull%d_%d" % (last, d))
-        empty(last, [0], bank, 0)
-        front_bank = new_bank([1], 2)
-        fetch_pull(last, [1], 0, front_bank, 0, "pull_front")
-        clip_and_add(last - 1, 0, False)
-        fetch_pull(last, [1], 1, front_bank, 1, slot(last - 1, 0))
-        clip_and_add(last - 1, 1, True)
-        back_bank = new_bank([1], 2)
-        fetch_pull(last, [1], 2, back_bank, 0, slot(last - 1, 1))
-        hand_out(last - 1, slice(0, V))
-        clipped = new_clipped()
-        clip(clipped[:], turned[last, 0][:], 0)
-        fetch_pull(last, [1], 3, back_bank, 1, slot(last, 0))
-        for d in range(D):
-            turn(total[last][:, 0], clipped[:, d], False, d == D - 1)
-        hand_out(last, slice(0, P))
+        slab[last] = keep.tile([P, D, V], F32, name="slab", tag=tags[last])
+        front_total = new_total([0])
+        for first in (0, 2):
+            bank = [new_bank(first // 2, 2)]
+            for place in range(2):
+                fetch_pull(last, [0], first + place, bank, place)
+            clip_on_scalar([0], bank, [front_total[:, 0]], first == 0, first == 2)
+        end_banks = []
+        for first in (0, 2):
+            bank = new_bank(first // 2, 2)
+            for place in range(2):
+                fetch_pull(last, [1], first + place, [bank], place)
+            end_banks.append(bank)
 
-        end_clipped = keep.tile([P, D, P], F32, name="end_clipped", tag="y%d" % last)
-        clip(end_clipped[:, :2], front_bank[:, 0], 1)
-        clip(end_clipped[:, 2:], back_bank[:, 0], 1)
-        end_total = psum.tile([P, P], F32, name="end_total", tag="rows", bufs=ROW_BANKS)
-        for d in range(D):
-            turn(end_total[:], end_clipped[:, d], d == 0, d == D - 1)
+        end_clipped = keep.tile([P, D, P], F32, name="end_clipped")
+        end_total = new_total([1])
+        for i, bank in enumerate(end_banks):
+            nc.vector.tensor_scalar(end_clipped[:, 2 * i : 2 * i + 2], bank[:], span[:, 1:2], 0.0, ALU.min, ALU.max)
+            add_up(end_total[:, 0], end_clipped[:, 2 * i : 2 * i + 2], 2, i == 0, i == 1)
 
-        regroup(1, slice(0, 2))
-        regroup(0, slice(0, PACK))
+        for h in both:
+            regroup(h, slice(0, 2))
+        hand_out(last - 1, flat(total[last - 1]), slice(0, V))
+        hand_out(last, front_total[:, 0], slice(0, P))
+        regroup(0, slice(2, PACK))
         nc.vector.tensor_copy(out_grouped[1][:, :, last - 1], result[:, last - 1, P:])
-        for out in (out_grouped[1][:, :, last], result[:, last, P:]):
-            nc.vector.scalar_tensor_tensor(out, end_total[:], 1.0 / D, centre[last][:, P:], ALU.mult, ALU.add)
-        nc.sync.dma_start(out_rows[:, last, P:], result[:, last, P:])
-        quantise_result(1)
+        finish(out_grouped[1][:, :, last], end_total[:, 0], last, slice(P, V))
         quantise_result(0)
+        hand_out(last, end_total[:, 0], slice(P, V))
+        quantise_result(1)
 
         for q in range(QUADRANTS):
             queue = nc.scalar if q % 2 == 0 else nc.sync

@@ -23,7 +23,7 @@ PACK = 4
 HALVES = V // P
 QUADRANTS = 4
 PER_COLUMN = 16
-ROW_BANKS = 5
+ROW_BANKS = 6
 
 
 def tile_picked_huber_none_po_kernel(
@@ -49,10 +49,10 @@ def tile_picked_huber_none_po_kernel(
             )
 
         w_rows = w1.rearrange("(p j) c -> p j c", j=PACK)
-        w_lo = keep.tile([P, PACK, N // 2], F32, name="w_lo")
-        w_hi = keep.tile([P, PACK, N // 2], F32, name="w_hi")
-        nc.sync.dma_start(w_lo[:], w_rows[:, :, : N // 2])
-        nc.sync.dma_start(w_hi[:], w_rows[:, :, N // 2 :])
+        w_lo = keep.tile([P, 2, N], F32, name="w_lo")
+        w_hi = keep.tile([P, 2, N], F32, name="w_hi")
+        nc.sync.dma_start(w_lo[:], w_rows[:, :2])
+        nc.sync.dma_start(w_hi[:], w_rows[:, 2:])
 
         cen_sb = keep.tile([P, V // PER_COLUMN], U16, name="cen_sb")
         nc.sync.dma_start(cen_sb[:], cen)
@@ -70,6 +70,9 @@ def tile_picked_huber_none_po_kernel(
         span = keep.tile([P, HALVES], F32, name="span")
         nc.scalar.activation(span[:], upper[:], COPY, scale=2.0)
 
+        span_rows = keep.tile([P, V], F32, name="span_rows")
+        nc.scalar.activation(span_rows[:], bound_rows[:], RELU, scale=2.0)
+
         ident = keep.tile([P, P], F32, name="ident")
         make_identity(nc, ident[:])
 
@@ -80,10 +83,10 @@ def tile_picked_huber_none_po_kernel(
 
         w_grouped = keep.tile([P, PACK, P, PACK], BF16, name="w_grouped", align_bytes=64)
         w_dealt = w_grouped[:].rearrange("p t m j -> p m t j")
-        nc.scalar.copy(w_dealt[:, : P // 2], w_lo[:].rearrange("p j (m t) -> p m t j", t=PACK))
+        nc.scalar.copy(w_dealt[:, :, :, :2], w_lo[:].rearrange("p j (m t) -> p m t j", t=PACK))
         w_hi_dealt = w_hi[:].rearrange("p j (m t) -> p m t j", t=PACK)
-        nc.vector.tensor_copy(w_dealt[:, P // 2 :, 0], w_hi_dealt[:, :, 0])
-        nc.scalar.copy(w_dealt[:, P // 2 :, 1:], w_hi_dealt[:, :, 1:])
+        nc.vector.tensor_copy(w_dealt[:, :, 0, 2:], w_hi_dealt[:, :, 0])
+        nc.scalar.copy(w_dealt[:, :, 1:, 2:], w_hi_dealt[:, :, 1:])
 
         w_codes = keep.tile([P, N], U32, name="w_codes", align_bytes=64)
         w_scales = keep.tile([P, N], U8, name="w_scales", align_bytes=64)
@@ -123,7 +126,6 @@ def tile_picked_huber_none_po_kernel(
         last = PACK - 1
         both = list(range(HALVES))
         floor, total, slab = {}, {}, {}
-        out_grouped = [keep.tile([P, P, PACK], BF16, name="out_grouped%d" % h, align_bytes=64) for h in both]
 
         def turn(bank_part, rows, start, stop):
             nc.tensor.matmul(bank_part, rows, ident[:], start=start, stop=stop, is_transpose=True)
@@ -147,11 +149,14 @@ def tile_picked_huber_none_po_kernel(
             for j in range(count):
                 turn(acc, clipped[:, j], start and j == 0, stop and j == count - 1)
 
-        def clip_on_scalar(halves, banks, accs, start, stop):
+        def clip_on_scalar(halves, banks, accs, start, stop, final=False):
             count = banks[0].shape[1]
             rooms = []
             for i, h in enumerate(halves):
-                room = work.tile([P, count, P], F32, name="room", bufs=4)
+                if final:
+                    room = keep.tile([P, count, P], F32, name="final_room%d" % h, align_bytes=64)
+                else:
+                    room = work.tile([P, count, P], F32, name="room", bufs=4)
                 nc.scalar.activation(room[:], banks[i][:], RELU, bias=span[:, h : h + 1], scale=-1.0)
                 rooms.append(room)
             for i, h in enumerate(halves):
@@ -182,62 +187,68 @@ def tile_picked_huber_none_po_kernel(
                 scales=out_scales[:, targets],
                 in_=out_grouped[h][:].rearrange("p v t -> p (v t)"),
             )
-            nc.sync.dma_start(out_words[:, targets], out_codes[:, targets].bitcast(I32))
 
         def flat(acc):
             return acc[:].rearrange("p h v -> p (h v)")
 
-        tags = ["slab_a", "slab_b", "slab_c", "slab_a"]
-        first_floor = keep.tile([P, V], F32, name="first_floor", tag="slab_c")
+        first_floor = keep.tile([P, V], F32, name="first_floor")
         fetch_floor(0, first_floor[:])
-        for t in range(last):
-            slab[t] = keep.tile([P, D + 1, V], F32, name="slab", tag=tags[t])
+        for t in range(PACK):
+            slab[t] = keep.tile([P, D + 1, V], F32, name="slab%d" % t)
             total[t] = new_total(both)
             accs = [total[t][:, h] for h in both]
             bank = [new_bank(h, 2) for h in both]
             for d in (0, 1):
                 fetch_pull(t, both, d, bank, d)
-            clip_on_scalar(both, bank, accs, True, False)
-            bank = [new_bank(h, 2) for h in both]
-            fetch_pull(t, both, 2, bank, 0)
             if t == 0:
-                fetch_floor(1, slab[0][:, D])
-            fetch_pull(t, both, 3, bank, 1)
-            if t > 0:
+                floor_bank = psum.tile([P, HALVES, P], F32, name="floor_bank", tag="rows", bufs=ROW_BANKS)
+                for h in both:
+                    turn(floor_bank[:, h], floor[0][:, h * P : (h + 1) * P], True, True)
+                floor_turned = keep.tile([P, HALVES, P], F32, name="floor_turned")
+                nc.scalar.activation(floor_turned[:], floor_bank[:], COPY, scale=float(D))
+                for h in both:
+                    turn(accs[h], floor_turned[:, h], h == 0, False)
+            clip_on_scalar(both, bank, accs, t > 0, t == last, t == last)
+            if t == 1:
+                nc.scalar.activation(result[:, 0], flat(total[0]), COPY, scale=1.0 / D)
+                nc.sync.dma_start(out_rows[:, 0], result[:, 0])
+            if t < last:
+                bank = [new_bank(h, 2) for h in both]
+                fetch_pull(t, both, 2, bank, 0)
                 fetch_floor(t + 1, slab[t][:, D])
-                hand_out(t - 1, flat(total[t - 1]), slice(0, V))
-            clip_on_scalar(both, bank, accs, False, True)
+                fetch_pull(t, both, 3, bank, 1)
+                clip_on_scalar(both, bank, accs, False, True)
 
-        slab[last] = keep.tile([P, D, V], F32, name="slab", tag=tags[last])
-        front_total = new_total([0])
-        for first in (0, 2):
-            bank = [new_bank(first // 2, 2)]
-            for place in range(2):
-                fetch_pull(last, [0], first + place, bank, place)
-            clip_on_scalar([0], bank, [front_total[:, 0]], first == 0, first == 2)
-        end_banks = []
-        for first in (0, 2):
-            bank = new_bank(first // 2, 2)
-            for place in range(2):
-                fetch_pull(last, [1], first + place, [bank], place)
-            end_banks.append(bank)
+        for d in (2, 3):
+            nc.vector.tensor_tensor(slab[last][:, d], y[last][:].indirect(pos_sb[d][:]), floor[last], ALU.subtract)
+        partial = floor[last]
+        for d in (2, 3):
+            clipped_rows = keep.tile([P, V], F32, name="clipped_rows%d" % d)
+            nc.vector.scalar_tensor_tensor(clipped_rows[:], slab[last][:, d], 0.0, span_rows[:], ALU.max, ALU.min)
+            summed = keep.tile([P, V], F32, name="summed%d" % d)
+            nc.vector.scalar_tensor_tensor(summed[:], clipped_rows[:], 1.0 / D, partial, ALU.mult, ALU.add)
+            partial = summed[:]
+        floor[last] = partial
 
-        end_clipped = keep.tile([P, D, P], F32, name="end_clipped")
-        end_total = new_total([1])
-        for i, bank in enumerate(end_banks):
-            nc.vector.tensor_scalar(end_clipped[:, 2 * i : 2 * i + 2], bank[:], span[:, 1:2], 0.0, ALU.min, ALU.max)
-            add_up(end_total[:, 0], end_clipped[:, 2 * i : 2 * i + 2], 2, i == 0, i == 1)
-
+        for t in range(1, last):
+            hand_out(t, flat(total[t]), slice(0, V))
+        out_grouped = [
+            keep.tile([P, P, PACK], BF16, name="out_grouped%d" % h, tag="final_room%d" % h, align_bytes=64)
+            for h in both
+        ]
         for h in both:
             regroup(h, slice(0, 2))
-        hand_out(last - 1, flat(total[last - 1]), slice(0, V))
-        hand_out(last, front_total[:, 0], slice(0, P))
+        for h in both:
+            finish(result[:, last, h * P : (h + 1) * P], total[last][:, h], last, slice(h * P, (h + 1) * P))
+        nc.sync.dma_start(out_rows[:, last], result[:, last])
         regroup(0, slice(2, PACK))
-        nc.vector.tensor_copy(out_grouped[1][:, :, last - 1], result[:, last - 1, P:])
-        finish(out_grouped[1][:, :, last], end_total[:, 0], last, slice(P, V))
-        quantise_result(0)
-        hand_out(last, end_total[:, 0], slice(P, V))
+        nc.vector.tensor_copy(
+            out_grouped[1][:, :, 2:].rearrange("p (c i) t -> p c t i", i=4),
+            result[:, 2:, P:].rearrange("p t (c i) -> p c t i", i=4),
+        )
         quantise_result(1)
+        quantise_result(0)
+        nc.sync.dma_start(out_words, out_codes[:].bitcast(I32))
 
         for q in range(QUADRANTS):
             queue = nc.scalar if q % 2 == 0 else nc.sync

@@ -23,7 +23,7 @@ PACK = 4
 HALVES = V // P
 QUADRANTS = 4
 PER_COLUMN = 16
-ROW_BANKS = 6
+ROW_BANKS = 4
 
 
 def tile_picked_huber_none_po_kernel(
@@ -132,7 +132,9 @@ def tile_picked_huber_none_po_kernel(
 
         def fetch_floor(t, out):
             floor[t] = out
-            nc.vector.tensor_tensor(out, y[t][:].indirect(cen_sb[:]), bound_rows[:], ALU.subtract)
+            for part in ([slice(0, P), slice(P, V)] if t == 0 else [slice(0, V)]):
+                columns = slice(part.start // PER_COLUMN, part.stop // PER_COLUMN)
+                nc.vector.tensor_tensor(out[:, part], y[t][:].indirect(cen_sb[:, columns]), bound_rows[:, part], ALU.subtract)
 
         def new_bank(tag, count):
             return psum.tile([P, count, P], F32, name="pull_bank", tag="pulls%d" % tag, bufs=1)
@@ -141,7 +143,16 @@ def tile_picked_huber_none_po_kernel(
             targets = slice(halves[0] * P, (halves[-1] + 1) * P)
             columns = slice(targets.start // PER_COLUMN, targets.stop // PER_COLUMN)
             pull = slab[t][:, d, targets]
-            nc.vector.tensor_tensor(pull, y[t][:].indirect(pos_sb[d][:, columns]), floor[t][:, targets], ALU.subtract)
+            if t == 0 and d == 0:
+                for h in both:
+                    nc.vector.tensor_tensor(
+                        pull[:, h * P : (h + 1) * P],
+                        y[t][:].indirect(pos_sb[d][:, h * 8 : (h + 1) * 8]),
+                        floor[t][:, h * P : (h + 1) * P],
+                        ALU.subtract,
+                    )
+            else:
+                nc.vector.tensor_tensor(pull, y[t][:].indirect(pos_sb[d][:, columns]), floor[t][:, targets], ALU.subtract)
             for i, h in enumerate(halves):
                 turn(banks[i][:, place], slab[t][:, d, h * P : (h + 1) * P], True, True)
 
@@ -149,18 +160,15 @@ def tile_picked_huber_none_po_kernel(
             for j in range(count):
                 turn(acc, clipped[:, j], start and j == 0, stop and j == count - 1)
 
-        def clip_on_scalar(halves, banks, accs, start, stop, final=False):
+        def clip_on_scalar(halves, banks, accs, start, stop):
             count = banks[0].shape[1]
             rooms = []
             for i, h in enumerate(halves):
-                if final:
-                    room = keep.tile([P, count, P], F32, name="final_room%d" % h, align_bytes=64)
-                else:
-                    room = work.tile([P, count, P], F32, name="room", bufs=4)
+                room = work.tile([P, count, P], F32, name="room", bufs=2, align_bytes=64)
                 nc.scalar.activation(room[:], banks[i][:], RELU, bias=span[:, h : h + 1], scale=-1.0)
                 rooms.append(room)
             for i, h in enumerate(halves):
-                clipped = work.tile([P, count, P], F32, name="clipped", bufs=6)
+                clipped = work.tile([P, count, P], F32, name="clipped", bufs=8)
                 nc.scalar.activation(clipped[:], rooms[i][:], RELU, bias=span[:, h : h + 1], scale=-1.0)
                 add_up(accs[i], clipped, count, start and i == 0, stop and i == len(halves) - 1)
 
@@ -208,16 +216,16 @@ def tile_picked_huber_none_po_kernel(
                 nc.scalar.activation(floor_turned[:], floor_bank[:], COPY, scale=float(D))
                 for h in both:
                     turn(accs[h], floor_turned[:, h], h == 0, False)
-            clip_on_scalar(both, bank, accs, t > 0, t == last, t == last)
-            if t == 1:
-                nc.scalar.activation(result[:, 0], flat(total[0]), COPY, scale=1.0 / D)
-                nc.sync.dma_start(out_rows[:, 0], result[:, 0])
+            clip_on_scalar(both, bank, accs, t > 0, t == last)
             if t < last:
-                bank = [new_bank(h, 2) for h in both]
+                bank = [new_bank(2 + h, 2) for h in both]
                 fetch_pull(t, both, 2, bank, 0)
                 fetch_floor(t + 1, slab[t][:, D])
                 fetch_pull(t, both, 3, bank, 1)
                 clip_on_scalar(both, bank, accs, False, True)
+            if t == 1:
+                nc.scalar.activation(result[:, 0], flat(total[0]), COPY, scale=1.0 / D)
+                nc.sync.dma_start(out_rows[:, 0], result[:, 0])
 
         for d in (2, 3):
             nc.vector.tensor_tensor(slab[last][:, d], y[last][:].indirect(pos_sb[d][:]), floor[last], ALU.subtract)
@@ -233,7 +241,7 @@ def tile_picked_huber_none_po_kernel(
         for t in range(1, last):
             hand_out(t, flat(total[t]), slice(0, V))
         out_grouped = [
-            keep.tile([P, P, PACK], BF16, name="out_grouped%d" % h, tag="final_room%d" % h, align_bytes=64)
+            work.tile([P, P, PACK], BF16, name="out_grouped%d" % h, tag="room", bufs=2, align_bytes=64)
             for h in both
         ]
         for h in both:
@@ -241,13 +249,13 @@ def tile_picked_huber_none_po_kernel(
         for h in both:
             finish(result[:, last, h * P : (h + 1) * P], total[last][:, h], last, slice(h * P, (h + 1) * P))
         nc.sync.dma_start(out_rows[:, last], result[:, last])
-        regroup(0, slice(2, PACK))
-        nc.vector.tensor_copy(
-            out_grouped[1][:, :, 2:].rearrange("p (c i) t -> p c t i", i=4),
-            result[:, 2:, P:].rearrange("p t (c i) -> p c t i", i=4),
-        )
-        quantise_result(1)
-        quantise_result(0)
+        for h in both:
+            nc.vector.tensor_copy(
+                out_grouped[h][:, :, 2:].rearrange("p (c i) t -> p c t i", i=4),
+                result[:, 2:, h * P : (h + 1) * P].rearrange("p t (c i) -> p c t i", i=4),
+            )
+        for h in both:
+            quantise_result(h)
         nc.sync.dma_start(out_words, out_codes[:].bitcast(I32))
 
         for q in range(QUADRANTS):

@@ -41,7 +41,7 @@ def tile_picked_huber_none_po_kernel(
         nc.sync.dma_start(offs_sb[:], offs)
 
         x_scale_table = keep.tile([P, T], U8, name="x_scale_table", align_bytes=64)
-        nc.gpsimd.memset(x_scale_table[:].bitcast(I32), 0)
+        nc.vector.memset(x_scale_table[:].bitcast(I32), 0)
         for q in range(QUADRANTS):
             nc.sync.dma_start(
                 x_scale_table[32 * q : 32 * q + 4, :].bitcast(I32),
@@ -83,10 +83,13 @@ def tile_picked_huber_none_po_kernel(
 
         w_grouped = keep.tile([P, PACK, P, PACK], BF16, name="w_grouped", align_bytes=64)
         w_dealt = w_grouped[:].rearrange("p t m j -> p m t j")
-        nc.scalar.copy(w_dealt[:, :, :, :2], w_lo[:].rearrange("p j (m t) -> p m t j", t=PACK))
+        w_lo_dealt = w_lo[:].rearrange("p j (m t) -> p m t j", t=PACK)
+        nc.scalar.copy(w_dealt[:, :, :2, :2], w_lo_dealt[:, :, :2])
+        nc.gpsimd.tensor_copy(w_dealt[:, :, 2:, :2], w_lo_dealt[:, :, 2:])
         w_hi_dealt = w_hi[:].rearrange("p j (m t) -> p m t j", t=PACK)
         nc.vector.tensor_copy(w_dealt[:, :, 0, 2:], w_hi_dealt[:, :, 0])
-        nc.scalar.copy(w_dealt[:, :, 1:, 2:], w_hi_dealt[:, :, 1:])
+        nc.scalar.copy(w_dealt[:, :, 1, 2:], w_hi_dealt[:, :, 1])
+        nc.scalar.copy(w_dealt[:, :, 2:, 2:], w_hi_dealt[:, :, 2:])
 
         w_codes = keep.tile([P, N], U32, name="w_codes", align_bytes=64)
         w_scales = keep.tile([P, N], U8, name="w_scales", align_bytes=64)

@@ -70,6 +70,9 @@ def tile_picked_huber_none_po_kernel(
         span = keep.tile([P, HALVES], F32, name="span")
         nc.scalar.activation(span[:], upper[:], COPY, scale=2.0)
 
+        minus_all = keep.tile([P, HALVES], F32, name="minus_all")
+        nc.scalar.activation(minus_all[:], upper[:], COPY, scale=-float(D))
+
         span_rows = keep.tile([P, V], F32, name="span_rows")
         nc.scalar.activation(span_rows[:], bound_rows[:], RELU, scale=2.0)
 
@@ -139,6 +142,11 @@ def tile_picked_huber_none_po_kernel(
                 columns = slice(part.start // PER_COLUMN, part.stop // PER_COLUMN)
                 nc.vector.tensor_tensor(out[:, part], y[t][:].indirect(cen_sb[:, columns]), bound_rows[:, part], ALU.subtract)
 
+        def fetch_centre(t):
+            centre = keep.tile([P, V], F32, name="centre%d" % t)
+            nc.scalar.activation(centre[:], y[t][:].indirect(cen_sb[:]), COPY)
+            floor[t] = centre[:]
+
         def new_bank(tag, count):
             return psum.tile([P, count, P], F32, name="pull_bank", tag="pulls%d" % tag, bufs=1)
 
@@ -163,12 +171,12 @@ def tile_picked_huber_none_po_kernel(
             for j in range(count):
                 turn(acc, clipped[:, j], start and j == 0, stop and j == count - 1)
 
-        def clip_on_scalar(halves, banks, accs, start, stop):
+        def clip_on_scalar(halves, banks, accs, start, stop, top):
             count = banks[0].shape[1]
             rooms = []
             for i, h in enumerate(halves):
                 room = work.tile([P, count, P], F32, name="room", bufs=2, align_bytes=64)
-                nc.scalar.activation(room[:], banks[i][:], RELU, bias=span[:, h : h + 1], scale=-1.0)
+                nc.scalar.activation(room[:], banks[i][:], RELU, bias=top[:, h : h + 1], scale=-1.0)
                 rooms.append(room)
             for i, h in enumerate(halves):
                 clipped = work.tile([P, count, P], F32, name="clipped", bufs=8)
@@ -205,30 +213,28 @@ def tile_picked_huber_none_po_kernel(
         first_floor = keep.tile([P, V], F32, name="first_floor")
         fetch_floor(0, first_floor[:])
         for t in range(PACK):
-            slab[t] = keep.tile([P, D + 1, V], F32, name="slab%d" % t)
+            slab[t] = keep.tile([P, D, V], F32, name="slab%d" % t)
             total[t] = new_total(both)
             accs = [total[t][:, h] for h in both]
+            from_centre = 0 < t < last
+            top = upper if from_centre else span
+            if from_centre:
+                for h in both:
+                    turn(accs[h], minus_all[:, h : h + 1].to_broadcast([P, P]), h == 0, False)
             bank = [new_bank(h, 2) for h in both]
             for d in (0, 1):
                 fetch_pull(t, both, d, bank, d)
-            if t == 0:
-                floor_bank = psum.tile([P, HALVES, P], F32, name="floor_bank", tag="rows", bufs=ROW_BANKS)
-                for h in both:
-                    turn(floor_bank[:, h], floor[0][:, h * P : (h + 1) * P], True, True)
-                floor_turned = keep.tile([P, HALVES, P], F32, name="floor_turned")
-                nc.scalar.activation(floor_turned[:], floor_bank[:], COPY, scale=float(D))
-                for h in both:
-                    turn(accs[h], floor_turned[:, h], h == 0, False)
-            clip_on_scalar(both, bank, accs, t > 0, t == last)
+            clip_on_scalar(both, bank, accs, not from_centre, t == last, top)
             if t < last:
+                fetch_centre(t + 1)
                 bank = [new_bank(2 + h, 2) for h in both]
                 fetch_pull(t, both, 2, bank, 0)
-                fetch_floor(t + 1, slab[t][:, D])
+                if t + 1 == last:
+                    last_floor = keep.tile([P, V], F32, name="last_floor")
+                    nc.vector.tensor_tensor(last_floor[:], floor[last], bound_rows[:], ALU.subtract)
+                    floor[last] = last_floor[:]
                 fetch_pull(t, both, 3, bank, 1)
-                clip_on_scalar(both, bank, accs, False, True)
-            if t == 1:
-                nc.scalar.activation(result[:, 0], flat(total[0]), COPY, scale=1.0 / D)
-                nc.sync.dma_start(out_rows[:, 0], result[:, 0])
+                clip_on_scalar(both, bank, accs, False, True, top)
 
         for d in (2, 3):
             nc.vector.tensor_tensor(slab[last][:, d], y[last][:].indirect(pos_sb[d][:]), floor[last], ALU.subtract)
@@ -241,7 +247,7 @@ def tile_picked_huber_none_po_kernel(
             partial = summed[:]
         floor[last] = partial
 
-        for t in range(1, last):
+        for t in range(last):
             hand_out(t, flat(total[t]), slice(0, V))
         out_grouped = [
             work.tile([P, P, PACK], BF16, name="out_grouped%d" % h, tag="room", bufs=2, align_bytes=64)

from contextlib import ExitStack

import concourse.mybir as mybir
from concourse.masks import make_identity

K, T, S, V, N = 512, 1024, 512, 256, 512
D = 4
FLOPS = 2 * K * N * S

F32 = mybir.dt.float32
BF16 = mybir.dt.bfloat16
I32 = mybir.dt.int32
U32 = mybir.dt.uint32
U16 = mybir.dt.uint16
U8 = mybir.dt.uint8
FP8X4 = mybir.dt.float8_e4m3fn_x4
ALU = mybir.AluOpType
COPY = mybir.ActivationFunctionType.Copy
RELU = mybir.ActivationFunctionType.Relu

P = 128
PACK = 4
HALVES = V // P
QUADRANTS = 4
PER_COLUMN = 16
ROW_BANKS = 4


def tile_picked_huber_none_po_kernel(
    tc, x_words, x_scales, w1, bound, offs, cen, pos1, pos2, pos3, pos4, out_0, out_1, out_2
):
    nc = tc.nc
    with ExitStack() as ctx:
        keep = ctx.enter_context(tc.tile_pool(name="keep", bufs=1))
        work = ctx.enter_context(tc.tile_pool(name="work", bufs=2))
        psum = ctx.enter_context(tc.psum_pool(name="psum", bufs=1))

        x_word_table = keep.tile([P, T], I32, name="x_word_table", align_bytes=64)
        nc.sync.dma_start(x_word_table[:], x_words[0].rearrange("p n t -> p (n t)").bitcast(I32))
        offs_sb = keep.tile([P, S // PER_COLUMN], U16, name="offs_sb")
        nc.sync.dma_start(offs_sb[:], offs)

        x_scale_table = keep.tile([P, T], U8, name="x_scale_table", align_bytes=64)
        nc.vector.memset(x_scale_table[:].bitcast(I32), 0)
        for q in range(QUADRANTS):
            nc.sync.dma_start(
                x_scale_table[32 * q : 32 * q + 4, :].bitcast(I32),
                x_scales[0, 4 * q : 4 * q + 4, :].bitcast(I32),
            )

        w_rows = w1.rearrange("(p j) c -> p j c", j=PACK)
        w_lo = keep.tile([P, 2, N], F32, name="w_lo")
        w_hi = keep.tile([P, 2, N], F32, name="w_hi")
        nc.sync.dma_start(w_lo[:], w_rows[:, :2])
        nc.sync.dma_start(w_hi[:], w_rows[:, 2:])

        cen_sb = keep.tile([P, V // PER_COLUMN], U16, name="cen_sb")
        nc.sync.dma_start(cen_sb[:], cen)
        bound_rows = keep.tile([P, V], F32, name="bound_rows")
        nc.sync.dma_start(bound_rows[:], bound)
        pos_sb = []
        for d, pos in enumerate((pos1, pos2, pos3, pos4)):
            pos_list = keep.tile([P, V // PER_COLUMN], U16, name="pos_sb%d" % d)
            nc.sync.dma_start(pos_list[:], pos)
            pos_sb.append(pos_list)

        upper = keep.tile([P, HALVES], F32, name="upper")
        with nc.allow_non_contiguous_dma(reason="one bound a partition"):
            nc.sync.dma_start(upper[:], bound[0].rearrange("(h p) -> p h", p=P))
        span = keep.tile([P, HALVES], F32, name="span")
        nc.scalar.activation(span[:], upper[:], COPY, scale=2.0)

        minus_all = keep.tile([P, HALVES], F32, name="minus_all")
        nc.scalar.activation(minus_all[:], upper[:], COPY, scale=-float(D))

        span_rows = keep.tile([P, V], F32, name="span_rows")
        nc.scalar.activation(span_rows[:], bound_rows[:], RELU, scale=2.0)

        ident = keep.tile([P, P], F32, name="ident")
        make_identity(nc, ident[:])

        x_scales_picked = keep.tile([P, S], U8, name="x_scales_picked", align_bytes=64)
        x_words_picked = keep.tile([P, S], U32, name="x_words_picked", align_bytes=64)
        nc.vector.tensor_copy(x_words_picked[:], x_word_table[:].bitcast(U32).indirect(offs_sb[:]))
        nc.vector.tensor_copy(x_scales_picked[:], x_scale_table[:].indirect(offs_sb[:]))

        w_grouped = keep.tile([P, PACK, P, PACK], BF16, name="w_grouped", align_bytes=64)
        w_dealt = w_grouped[:].rearrange("p t m j -> p m t j")
        w_lo_dealt = w_lo[:].rearrange("p j (m t) -> p m t j", t=PACK)
        nc.scalar.copy(w_dealt[:, :, :2, :2], w_lo_dealt[:, :, :2])
        nc.gpsimd.tensor_copy(w_dealt[:, :, 2:, :2], w_lo_dealt[:, :, 2:])
        w_hi_dealt = w_hi[:].rearrange("p j (m t) -> p m t j", t=PACK)
        nc.vector.tensor_copy(w_dealt[:, :, 0, 2:], w_hi_dealt[:, :, 0])
        nc.scalar.copy(w_dealt[:, :, 1, 2:], w_hi_dealt[:, :, 1])
        nc.scalar.copy(w_dealt[:, :, 2:, 2:], w_hi_dealt[:, :, 2:])

        w_codes = keep.tile([P, N], U32, name="w_codes", align_bytes=64)
        w_scales = keep.tile([P, N], U8, name="w_scales", align_bytes=64)
        y = []
        for t in range(PACK):
            cols = slice(t * P, (t + 1) * P)
            nc.vector.quantize_mx(
                out=w_codes[:, cols].bitcast(FP8X4),
                scales=w_scales[:, cols],
                in_=w_grouped[:, t].rearrange("p m j -> p (m j)"),
            )
            y_t = keep.tile([P, S], F32, name="y%d" % t)
            if t == 0:
                pieces = [(slice(0, S // 2), nc.vector.tensor_copy), (slice(S // 2, S), nc.scalar.copy)]
            else:
                pieces = [(slice(0, S), nc.scalar.copy)]
            for entries, copy_out in pieces:
                y_bank = psum.tile([P, entries.stop - entries.start], F32, name="y_bank", tag="rows", bufs=ROW_BANKS)
                nc.tensor.matmul_mx(
                    out=y_bank[:],
                    lhsT=w_codes[:, cols].bitcast(FP8X4),
                    lhsT_scale=w_scales[:, cols],
                    rhs=x_words_picked[:, entries].bitcast(FP8X4),
                    rhs_scale=x_scales_picked[:, entries],
                    start=True,
                    stop=True,
                )
                copy_out(y_t[:, entries], y_bank[:])
            y.append(y_t)

        out_rows = out_0.rearrange("(p t) v -> p t v", t=PACK)
        out_words = out_1[0].rearrange("p v t -> p (v t)").bitcast(I32)
        result = keep.tile([P, PACK, V], F32, name="result")
        out_codes = keep.tile([P, V], U32, name="out_codes", align_bytes=64)
        out_scales = keep.tile([P, V], U8, name="out_scales", align_bytes=64)

        last = PACK - 1
        both = list(range(HALVES))
        floor, total, slab = {}, {}, {}

        def turn(bank_part, rows, start, stop):
            nc.tensor.matmul(bank_part, rows, ident[:], start=start, stop=stop, is_transpose=True)

        def fetch_floor(t, out):
            floor[t] = out
            for part in ([slice(0, P), slice(P, V)] if t == 0 else [slice(0, V)]):
                columns = slice(part.start // PER_COLUMN, part.stop // PER_COLUMN)
                nc.vector.tensor_tensor(out[:, part], y[t][:].indirect(cen_sb[:, columns]), bound_rows[:, part], ALU.subtract)

        def fetch_centre(t):
            centre = keep.tile([P, V], F32, name="centre%d" % t)
            nc.scalar.activation(centre[:], y[t][:].indirect(cen_sb[:]), COPY)
            floor[t] = centre[:]

        def new_bank(tag, count):
            return psum.tile([P, count, P], F32, name="pull_bank", tag="pulls%d" % tag, bufs=1)

        def fetch_pull(t, halves, d, banks, place):
            targets = slice(halves[0] * P, (halves[-1] + 1) * P)
            columns = slice(targets.start // PER_COLUMN, targets.stop // PER_COLUMN)
            pull = slab[t][:, d, targets]
            if t == 0 and d == 0:
                for h in both:
                    nc.vector.tensor_tensor(
                        pull[:, h * P : (h + 1) * P],
                        y[t][:].indirect(pos_sb[d][:, h * 8 : (h + 1) * 8]),
                        floor[t][:, h * P : (h + 1) * P],
                        ALU.subtract,
                    )
            else:
                nc.vector.tensor_tensor(pull, y[t][:].indirect(pos_sb[d][:, columns]), floor[t][:, targets], ALU.subtract)
            for i, h in enumerate(halves):
                turn(banks[i][:, place], slab[t][:, d, h * P : (h + 1) * P], True, True)

        def add_up(acc, clipped, count, start, stop):
            for j in range(count):
                turn(acc, clipped[:, j], start and j == 0, stop and j == count - 1)

        def clip_on_scalar(halves, banks, accs, start, stop, top):
            count = banks[0].shape[1]
            rooms = []
            for i, h in enumerate(halves):
                room = work.tile([P, count, P], F32, name="room", bufs=2, align_bytes=64)
                nc.scalar.activation(room[:], banks[i][:], RELU, bias=top[:, h : h + 1], scale=-1.0)
                rooms.append(room)
            for i, h in enumerate(halves):
                clipped = work.tile([P, count, P], F32, name="clipped", bufs=8)
                nc.scalar.activation(clipped[:], rooms[i][:], RELU, bias=span[:, h : h + 1], scale=-1.0)
                add_up(accs[i], clipped, count, start and i == 0, stop and i == len(halves) - 1)

        def new_total(halves):
            return psum.tile([P, len(halves), P], F32, name="total", tag="rows", bufs=ROW_BANKS)

        def finish(out, acc, t, targets):
            nc.vector.scalar_tensor_tensor(out, acc, 1.0 / D, floor[t][:, targets], ALU.mult, ALU.add)

        def hand_out(t, acc, targets):
            finish(result[:, t, targets], acc, t, targets)
            nc.sync.dma_start(out_rows[:, t, targets], result[:, t, targets])

        def regroup(h, blocks):
            nc.scalar.copy(
                out_grouped[h][:, :, blocks].rearrange("p (c i) t -> p c t i", i=4),
                result[:, blocks, h * P : (h + 1) * P].rearrange("p t (c i) -> p c t i", i=4),
            )

        def quantise_result(h):
            targets = slice(h * P, (h + 1) * P)
            nc.vector.quantize_mx(
                out=out_codes[:, targets].bitcast(FP8X4),
                scales=out_scales[:, targets],
                in_=out_grouped[h][:].rearrange("p v t -> p (v t)"),
            )

        def flat(acc):
            return acc[:].rearrange("p h v -> p (h v)")

        first_floor = keep.tile([P, V], F32, name="first_floor")
        fetch_floor(0, first_floor[:])
        for t in range(PACK):
            slab[t] = keep.tile([P, D, V], F32, name="slab%d" % t)
            total[t] = new_total(both)
            accs = [total[t][:, h] for h in both]
            from_centre = 0 < t < last
            top = upper if from_centre else span
            if from_centre:
                for h in both:
                    turn(accs[h], minus_all[:, h : h + 1].to_broadcast([P, P]), h == 0, False)
            bank = [new_bank(h, 2) for h in both]
            for d in (0, 1):
                fetch_pull(t, both, d, bank, d)
            clip_on_scalar(both, bank, accs, not from_centre, t == last, top)
            if t < last:
                fetch_centre(t + 1)
                bank = [new_bank(2 + h, 2) for h in both]
                fetch_pull(t, both, 2, bank, 0)
                if t + 1 == last:
                    last_floor = keep.tile([P, V], F32, name="last_floor")
                    nc.vector.tensor_tensor(last_floor[:], floor[last], bound_rows[:], ALU.subtract)
                    floor[last] = last_floor[:]
                fetch_pull(t, both, 3, bank, 1)
                clip_on_scalar(both, bank, accs, False, True, top)

        for d in (2, 3):
            nc.vector.tensor_tensor(slab[last][:, d], y[last][:].indirect(pos_sb[d][:]), floor[last], ALU.subtract)
        partial = floor[last]
        for d in (2, 3):
            clipped_rows = keep.tile([P, V], F32, name="clipped_rows%d" % d)
            nc.vector.scalar_tensor_tensor(clipped_rows[:], slab[last][:, d], 0.0, span_rows[:], ALU.max, ALU.min)
            summed = keep.tile([P, V], F32, name="summed%d" % d)
            nc.vector.scalar_tensor_tensor(summed[:], clipped_rows[:], 1.0 / D, partial, ALU.mult, ALU.add)
            partial = summed[:]
        floor[last] = partial

        for t in range(last):
            hand_out(t, flat(total[t]), slice(0, V))
        out_grouped = [
            work.tile([P, P, PACK], BF16, name="out_grouped%d" % h, tag="room", bufs=2, align_bytes=64)
            for h in both
        ]
        for h in both:
            regroup(h, slice(0, 2))
        for h in both:
            finish(result[:, last, h * P : (h + 1) * P], total[last][:, h], last, slice(h * P, (h + 1) * P))
        nc.sync.dma_start(out_rows[:, last], result[:, last])
        for h in both:
            nc.vector.tensor_copy(
                out_grouped[h][:, :, 2:].rearrange("p (c i) t -> p c t i", i=4),
                result[:, 2:, h * P : (h + 1) * P].rearrange("p t (c i) -> p c t i", i=4),
            )
        for h in both:
            quantise_result(h)
        nc.sync.dma_start(out_words, out_codes[:].bitcast(I32))

        for q in range(QUADRANTS):
            queue = nc.scalar if q % 2 == 0 else nc.sync
            queue.dma_start(
                out_2[0, 4 * q : 4 * q + 4, :].bitcast(I32),
                out_scales[32 * q : 32 * q + 4, :].bitcast(I32),
            )
